import numpy as np, ml_dtypes
CORES = [25,29,65,69,153,157,193,197]
N = 8
BF = ml_dtypes.bfloat16
def gentries(a):
    return np.ascontiguousarray(a.reshape(8, 16, -1).transpose(0, 2, 1)).reshape(8, -1)
def gtable(e):
    e = np.asarray(e); return np.ascontiguousarray(e.reshape(8, -1, 16).transpose(0, 2, 1)).reshape(128, -1).astype(np.int32)
W, B, E, SH, L, H = 3072, 256, 16, 4, 4, 2
R = L * B
def parts(rng):
    Y = rng.integers(0, 256, (N, 8, 16, W)); X = rng.integers(0, 256, (N, 8, 16, R)); m = rng.integers(0, W, (N, 8, R))
    lev = np.arange(B, R) // B; h = []
    for k in range(2):
        at = np.where(rng.random((N, 8, R - B)) < 0.5, 0, (lev * rng.random((N, 8, R - B))).astype(np.int64))
        h.append(rng.integers(0, H + 1, (N, 8, R - B)) * R + at * B + rng.integers(0, B, (N, 8, R - B)))
    a, b = rng.integers(0, W, (N, 8, B)), rng.integers(0, W, (N, 8, B)); far = rng.random((N, 8, B)) < 0.7
    lo = np.where(far, rng.integers(0, W // 4, (N, 8, B)), np.minimum(a, b)); hi = np.where(far, rng.integers(3 * W // 4, W, (N, 8, B)), np.maximum(a, b))
    return Y, X, h[0], h[1], m, lo, hi
def pack(Y, X, a, b, m, lo, hi):
    return {"ytab": np.ascontiguousarray(Y.reshape(N, 128, W)).astype(np.float32).astype(BF), "xrow": np.ascontiguousarray(X.reshape(N, 128, R)).astype(np.float32).astype(BF),
            "ha": np.stack([gtable(v) for v in a]), "hb": np.stack([gtable(v) for v in b]), "home": np.stack([gtable(v) for v in m]), "lo0": np.stack([gtable(v) for v in lo]), "hi0": np.stack([gtable(v) for v in hi])}
def setup_inputs(rng):
    return pack(*parts(rng))
def setup_inputs_ties(rng):
    Y, X, a, b, m, lo, hi = parts(rng)
    Y = np.take_along_axis(rng.integers(0, 256, (N, 8, 16, 4)), rng.integers(0, 4, (N, 8, 1, W)), 3)
    Y[:, 0] = Y[:, 0, :, :1]
    hi = np.where(rng.random(hi.shape) < 0.2, np.minimum(lo + rng.integers(0, E, hi.shape), W - 1), hi)
    m[:, :, :B] = (lo + hi) >> 1
    return pack(Y, X, a, b, m, lo, hi)
def setup_inputs_narrow(rng):
    Y, X, a, b, m, lo, hi = parts(rng)
    lo = rng.integers(0, W - 1, lo.shape); lo[:, :4] = rng.integers(0, W - 1024, (1, 4, 1)) + rng.integers(0, 40, (N, 4, B))
    hi = np.minimum(lo + rng.choice(np.array([0, 1, 2, E - 1, E, E + 1, 2 * E + 1, 300]), lo.shape), W - 1)
    for k, (p, q) in enumerate(((0, 0), (W - 1, W - 1), (0, W - 1), (W - 2, W - 1), (0, 1))): lo[:, 3:, k] = p; hi[:, 3:, k] = q
    t = rng.random((N, 5, R - B)) < 0.2
    a[:, 3:] = np.where(t, 1, a[:, 3:]); b[:, 3:] = np.where(t, H * R, b[:, 3:])
    lo[:, 7] = (E * np.arange(B)) % W; hi[:, 7] = np.minimum(lo[:, 7] + E, W - 1)
    o = np.arange(R - B); a[:, 7] = o; b[:, 7] = o + (o % B < B - 1)
    return pack(Y, X, a, b, m, lo, hi)
def setup_inputs_alike(rng):
    Y, X, a, b, m, lo, hi = parts(rng); lev = np.arange(B, R) // B
    v = a.reshape(N, 8, L - 1, B); a = np.where((np.arange(8) % 2 == 0)[None, :, None, None], v[..., :1], v).reshape(N, 8, R - B)
    a[:, 4] = rng.integers(0, H + 1, (N, 1)) * R + rng.integers(0, B, (N, 1))
    b[:, 1] = np.where(rng.random((N, R - B)) < 0.5, a[:, 1], b[:, 1]); b[:, 2] = a[:, 2]
    a[:, 3] = a[:, 3] % R; b[:, 3] = b[:, 3] % R
    a[:, 5] = a[:, 5] % R + H * R; b[:, 5] = b[:, 5] % R + H * R
    for w in (a, b): w[:, 7] = rng.integers(0, H + 1, (N, R - B)) * R + np.where(rng.random((N, R - B)) < 0.5, 0, B * lev - 1)
    return pack(Y, X, a, b, m, lo, hi)
def setup_inputs_far(rng):
    Y, X, a, b, m, lo, hi = parts(rng)
    Y = 255 * rng.integers(0, 2, Y.shape); X = 255 * rng.integers(0, 2, (N, 8, 1, R)) + np.zeros((1, 1, 16, 1), np.int64); m = (W - 1) * rng.integers(0, 2, m.shape)
    Y[:, 0] = 255; X[:, 0] = 0; Y[:, 1] = 0; X[:, 1] = 255; lo[:, :, :8] = 0; m[:, :, :4] = W - 1; m[:, :, 4:8] = 0
    for i, p, q, c in ((8, W - 1, W - 1, 0), (12, W - 16, W - 1, 0), (16, 0, 31, W - 1), (20, 1, 15, W - 1)): lo[:, :2, i:i + 4] = p; hi[:, :2, i:i + 4] = q; m[:, :2, i:i + 4] = c
    a[:, 1, ::B] = 8; b[:, 1, ::B] = H * R + 9
    Y[:, 2] = rng.integers(0, 2, (N, 16, W)); X[:, 2] = 255; hi[:, 2] = np.minimum(lo[:, 2] + 2 * E, W - 1)
    return pack(Y, X, a, b, m, lo, hi)
def setup_inputs_spread(rng):
    Y, X, a, b, m, lo, hi = parts(rng); lev = np.arange(B, R) // B
    Y = (np.exp2(rng.integers(1, 9, (N, 8, 1, W))) * rng.random(Y.shape)).astype(np.int64); X = (np.exp2(rng.integers(1, 9, (N, 8, 1, R))) * rng.random(X.shape)).astype(np.int64)
    a = (a // R) * R + (B * lev * rng.random(a.shape) ** 3).astype(np.int64); m = (W * rng.random(m.shape) ** 2).astype(np.int64)
    return pack(Y, X, a, b, m, lo, hi)
def check_inputs(d):
    bad = []
    for k in ("ytab", "xrow"):
        v = np.asarray(d[k]).astype(np.float32)
        if not np.all((v >= 0) & (v <= 255) & (v == np.floor(v))): bad.append("whole numbers of " + k)
    for k in ("home", "lo0", "hi0"):
        if np.min(d[k]) < 0 or np.max(d[k]) >= W: bad.append("range of " + k)
    if np.any(d["lo0"] > d["hi0"]): bad.append("lo0 over hi0")
    lev = np.arange(B, R) // B
    for k in ("ha", "hb"):
        h = np.stack([gentries(v) for v in d[k]]).astype(np.int64)
        if np.min(h) < 0 or np.max(h) >= (H + 1) * R or np.any(h % R >= B * lev): bad.append("rows that " + k + " names")
    return bad
def reference(ytab, xrow, ha, hb, home, lo0, hi0):
    Y = ytab.astype(np.float32).astype(np.int32).reshape(N, 8, 16, W); X = xrow.astype(np.float32).astype(np.int32).reshape(N, 8, 16, R)
    a, b, m, first, last = [np.stack([gentries(v) for v in t]).astype(np.int64) for t in (ha, hb, home, lo0, hi0)]
    e = np.arange(E); wins = []
    for ps in range(2):
        arg = np.zeros((N, 8, R), np.int64)
        for l in range(L):
            s = l * B
            if l == 0: lo, hi = first, last
            else:
                known = np.concatenate([np.roll(arg, -k, axis=0) for k in range(H + 1)], axis=2)
                u = np.take_along_axis(known, a[:, :, s - B:s], 2); v = np.take_along_axis(known, b[:, :, s - B:s], 2)
                lo, hi = np.minimum(u, v), np.maximum(u, v)
            j = lo[..., None] + (((hi - lo)[..., None] * e) >> SH)
            y = np.take_along_axis(Y, j.reshape(N, 8, 1, B * E), 3).reshape(N, 8, 16, B, E)
            cost = np.add.reduce(np.abs(X[..., s:s + B, None] - y), axis=2) + (np.abs(j - m[:, :, s:s + B, None]) >> 4)
            k = np.argmin(cost, axis=3)
            arg[:, :, s:s + B] = np.take_along_axis(j, k[..., None], 3)[..., 0]
        X = np.abs(X - np.take_along_axis(Y, arg[:, :, None, :], 3))
        wins.append(arg)
    both = np.concatenate(wins, axis=2)
    return {"argm": np.stack([gtable(v) for v in both]).astype(np.float32), "xo": X.reshape(N, 128, R).astype(np.float32)}

@@ -1,0 +1,420 @@
+from concourse.bass import DstId, RemoteDMATransfer
+from concourse.mybir import AluOpType as A, ActivationFunctionType as F
+
+NBS = [2, 2, 2, 2, 2, 2, 2, 2]
+ORDER = """
+lm.0 ex.0 of.0 ib.0 ha.0 zs.0 g0.0 hf.0 ni.0 g1.0 ik.0 xb.0 p0.0 jf.0 p1.0 a0.0 d3.0 d2.0 d4.0 d5.0 d6.0 a3.0 a1.0 q0.0
+d7.0 a2.0 a4.0 h1.0 ks.0 q1.0 h2.0 a5.0 r1.0 h6.0 q2.0 a6.0 h3.0 a7.0 h5.0 s9.0 s0.0 r2.0 s12.0 h7.0 s11.0 h4.0 s3.0
+s13.0 s15.0 hC.0 s10.0 h9.0 q3.0 r3.0 w1.0 w2.0 s7.0 w3.0 s1.0 s14.0 w4.0 wo.0 s2.0 h8.0 ld.0 s5.0 la.0 s8.0
+p1.1 s6.0 hA.0 a1.1 s4.0 hD.0 hB.0 d6.1 d5.1 a6.1 p0.1 d3.1 m1.0 m2.0 d2.1 d4.1 a0.1 m0.0 q0.1 e0.0 a5.1 d7.1 e2.0
+a3.1 a2.1 q1.1 ks.1 r1.1 a4.1 q2.1 e1.0 a7.1 r2.1 q3.1 ga.2 gb.2 r3.1 w1.1 pu.2 pv.2 us.2 w2.1 ll.2 ar.0 hh.2 w3.1 w4.1
+ex.2 of.2 ha.2 g0.2 wo.1 g1.2 d2.2 p0.2 d3.2 d4.2 p1.2 hf.2 a2.2 jf.2 a0.2 a1.2 d5.2 a3.2 a4.2 a5.2 d6.2 d7.2 q0.2
+ga.3 ks.2 gb.3 q1.2 q2.2 r1.2 ld.1 a6.2 pu.3 a7.2 r2.2 us.3 pv.3 ll.3 hh.3 q3.2 r3.2 la.1 w1.2 ex.3 w2.2 w3.2 w4.2 wo.2
+ld.2 ha.3 of.3 hf.3 la.2 jf.3 g0.3 p0.3 g1.3 d2.3 d4.3 a2.3 d3.3 a0.3 p1.3 d5.3 d6.3 a1.3 a3.3 d7.3 q0.3 q1.3 a4.3
+ks.3 a5.3 a6.3 q2.3 a7.3 ga.4 pu.4 r1.3 us.4 q3.3 gb.4 r2.3 r3.3 w1.3 pv.4 ll.4 hh.4 w2.3 w3.3 w4.3 ex.4 of.4 ha.4
+g0.4 g1.4 p0.4 wo.3 p1.4 d2.4 d4.4 jf.4 hf.4 d3.4 d5.4 a2.4 a0.4 d6.4 a1.4 a3.4 q0.4 q1.4 a4.4 ks.4 d7.4 r1.4 a5.4
+ld.3 q2.4 r2.4 a6.4 a7.4 q3.4 ga.5 gb.5 r3.4 w1.4 w2.4 pu.5 pv.5 w3.4 la.3 us.5 ll.5 w4.4 hh.5 ex.5 wo.4 ld.4 ha.5
+of.5 la.4 g0.5 hf.5 g1.5 jf.5 d2.5 p0.5 a2.5 d3.5 p1.5 a0.5 d4.5 d5.5 d6.5 a1.5 q0.5 a3.5 a4.5 a5.5 d7.5 ks.5 ga.6
+q1.5 q2.5 a6.5 r1.5 r2.5 pu.6 a7.5 gb.6 q3.5 r3.5 us.6 pv.6 ar.2 w1.5 ll.6 hh.6 w2.5 w3.5 ex.6 w4.5 of.6 wo.5 ha.6
+jf.6 g0.6 p0.6 d3.6 d4.6 d2.6 g1.6 a3.6 a0.6 p1.6 a1.6 hf.6 d5.6 d6.6 a2.6 a5.6 d7.6 q0.6 q1.6 a4.6 ks.6 a6.6 r1.6
+a7.6 q2.6 ld.5 r2.6 ga.7 q3.6 ar.4 gb.7 pu.7 pv.7 us.7 r3.6 la.5 w1.6 w2.6 w3.6 ll.7 hh.7 w4.6 ar.3 ex.7 ar.5 wo.6
+ar.6 ld.6 ha.7 of.7 hf.7 la.6 jf.7 g0.7 g1.7 d2.7 p0.7 d3.7 d5.7 a2.7 d4.7 d6.7 p1.7 a0.7 a1.7 a3.7 q0.7 a4.7 ks.7
+d7.7 a5.7 a6.7 q1.7 r1.7 a7.7 ar.1 q2.7 q3.7 r2.7 r3.7 w1.7 w2.7 w3.7 w4.7 ar.7 wo.7 ld.7 la.7
+"""
+CEN = 1536.0
+MAGIC = 1.5 * 2.0 ** 35
+
+
+def _sb(n, d):
+    return ("sbuf", [128, n], d)
+
+
+SCRATCH = {
+    "YT": _sb(3072, "bfloat16"), "X1": _sb(2048, "bfloat16"), "X2": _sb(1024, "bfloat16"),
+    "XO": _sb(1024, "float32"), "AR": _sb(128, "float32"),
+    "D0": _sb(4096, "bfloat16"), "D1": _sb(4096, "bfloat16"), "YG0": _sb(1536, "bfloat16"), "YG1": _sb(1536, "bfloat16"),
+    "OF0": _sb(256, "uint16"), "OF1": _sb(256, "uint16"), "JF0": _sb(256, "float16"), "JF1": _sb(256, "float16"),
+    "HF0": _sb(256, "float16"), "HF1": _sb(256, "float16"), "XZ": _sb(256, "float32"),
+    "W0": _sb(192, "float32"), "W1": _sb(192, "float32"), "GA": _sb(256, "float16"), "GB": _sb(256, "float16"),
+    "US": _sb(128, "float32"), "LH": _sb(512, "float16"),
+    "R0": _sb(64, "float32"), "R1": _sb(64, "float32"), "R2": _sb(64, "float32"), "R3": _sb(64, "float32"),
+    "T3": _sb(32, "float32"), "T4": _sb(16, "float32"), "T5": _sb(16, "float32"),
+    "WO": _sb(16, "uint16"), "LD": _sb(256, "bfloat16"),
+    "BR": _sb(32, "int32"), "BR16": _sb(32, "float16"), "HM": _sb(64, "int32"), "HM16": _sb(64, "float16"),
+    "HI": _sb(96, "int32"), "H1": _sb(96, "int32"), "H2": _sb(96, "int32"), "H3": _sb(96, "int32"), "H4": _sb(96, "int32"),
+    "HO": _sb(96, "uint16"), "HR": _sb(96, "float32"), "RD": _sb(1536, "bfloat16"), "MK": _sb(1536, "bfloat16"),
+    "PI": _sb(4, "int32"), "PJ": _sb(4, "int32"), "PC": _sb(4, "float32"), "AB": _sb(2, "float32"),
+    "J": _sb(144, "float32"), "J16": _sb(128, "float32"), "CJ": _sb(256, "float32"), "EJ": _sb(256, "float32"),
+    "EW": _sb(256, "float16"), "ED": _sb(256, "float16"), "E": _sb(256, "float16"),
+    "IH": _sb(128, "float16"), "IK": _sb(128, "float16"), "IB": _sb(128, "bfloat16"), "NI": _sb(128, "bfloat16"),
+    "BO": _sb(128, "bfloat16"), "ZS": _sb(144, "bfloat16"), "BG": _sb(8, "float16"), "I16": _sb(16, "float32"),
+}
+for _n in ("K0", "K1", "PU", "PV", "PZ", "PY", "PD0", "PD1"):
+    SCRATCH[_n] = ("psum", [128, 512], "float32")
+SEMAPHORES = ["cv", "ca", "cp", "cg", "lbr", "lhm", "ly", "lx0", "lhi", "lx1", "st", "sent"] + \
+             ["arr%d%d" % (s, l) for s in range(2) for l in range(3)]
+
+
+def routes(T, topo):
+    cores = list(T.cores)
+    n = len(cores)
+    taken = []
+    out = []
+    for r in range(n):
+        src = cores[r]
+        ways = []
+        for b in (1, 2):
+            dst = cores[(r - b) % n]
+            if topo.may_write(src, dst):
+                ways.append((dst, dst, b))
+                continue
+            cand = [c for c in topo.cores_of(src) if c not in cores and c not in taken and topo.may_write(c, dst)]
+            cand.sort(key=lambda c: (topo.die(c) != topo.die(src), c))
+            taken.append(cand[0])
+            ways.append((cand[0], dst, b))
+        out.append(ways)
+    return out
+
+
+def bits(engines):
+    m = 0
+    for e in engines:
+        m |= 1 << e
+    return m
+
+
+def first_hop_masks(src, ways, topo):
+    a, b = topo.engines(src, ways[0][0]), topo.engines(src, ways[1][0])
+    both = [e for e in a if e in b]
+    h = len(both) // 2
+    return [both[:h], both[h:2 * h]]
+
+
+def slot(T, s, l, b):
+    return T["W%d" % s][:, 48 * l + 16 * b:48 * l + 16 * b + 16]
+
+
+def relay_program(g, core, T, topo, src, ways, k):
+    _, dst, b = ways[k]
+    n_in = len(first_hop_masks(src, ways, topo)[k])
+    rid, pid = topo.addr(dst, core)
+    n_out = len(topo.engines(core, dst))
+    for l in range(3):
+        for s in range(2):
+            sem = T.sem["arr%d%d" % (s, l)]
+            g.wait_ge(sem, n_in)
+            g.remote_dma(slot(T, s, l, b), slot(T, s, l, b), sem, T.sem.sent, pid, rid, topo.mask(core, dst))
+    g.wait_ge(T.sem.sent, 6 * n_out)
+
+
+def rank_program(g, core, T, topo):
+    rank = T.rank_of(core)
+    plan = routes(T, topo)
+    cores = list(T.cores)
+    if rank is None:
+        for r, ways in enumerate(plan):
+            for k in range(2):
+                if ways[k][0] == core:
+                    relay_program(g, core, T, topo, cores[r], ways, k)
+        return
+
+    n_arr = 0
+    for r, ways in enumerate(plan):
+        for k in range(2):
+            first, dst, _ = ways[k]
+            if dst == core:
+                n_arr += len(first_hop_masks(cores[r], ways, topo)[k]) if first == dst else len(topo.engines(first, dst))
+    my_ways = plan[rank]
+    my_masks = first_hop_masks(core, my_ways, topo)
+
+    Q = {"v": g.vector, "a": g.scalar, "p": g.tensor, "g": g, "s": g.sync}
+    CS = {"v": "cv", "a": "ca", "p": "cp", "g": "cg"}
+    count = {"v": 0, "a": 0, "p": 0, "g": 0}
+    waited = {k: {} for k in Q}
+    last_w, readers, bank = {}, {}, {}
+    stores = [0]
+
+    def need(eng, deps):
+        best = {}
+        for (e, sem, val) in deps:
+            if e == "p" and eng == "p":
+                continue
+            best[sem] = max(best.get(sem, 0), val)
+        for sem, val in best.items():
+            if waited[eng].get(sem, 0) < val:
+                Q[eng].wait_ge(T.sem[sem], val)
+                waited[eng][sem] = val
+
+    def deps_of(eng, r, w, banks, extra):
+        deps = list(extra)
+        for k in r:
+            deps.append(last_w[k])
+        for k in w:
+            if k in last_w:
+                deps.append(last_w[k])
+            deps.extend(readers.get(k, []))
+        for k in banks:
+            for e, t in bank.get(k, {}).items():
+                if e != eng:
+                    deps.append(t)
+        return deps
+
+    def op(eng, fn, r=(), w=(), banks=(), extra=()):
+        need(eng, deps_of(eng, r, w, banks, extra))
+        count[eng] += 1
+        fn(Q[eng]).then_inc(T.sem[CS[eng]], 1)
+        tok = (eng, CS[eng], count[eng])
+        for k in r:
+            readers.setdefault(k, []).append(tok)
+        for k in w:
+            last_w[k] = tok
+            readers[k] = []
+        for k in banks:
+            bank.setdefault(k, {})[eng] = tok
+        return tok
+
+    def load(eng, out, in_, sem, total, key):
+        Q[eng].dma_start(out, in_).then_inc(T.sem[sem], 16)
+        last_w[key] = ("d", sem, total)
+
+    def store(eng, out, in_, r):
+        need(eng, deps_of(eng, r, (), (), ()))
+        Q[eng].dma_start(out, in_).then_inc(T.sem.st, 16)
+        stores[0] += 16
+
+    def ts(out, in0, s1, s2, op0, op1, r, w, banks=()):
+        if op1 is None:
+            return op("v", lambda q: q.tensor_scalar(out, in0, s1, None, op0), r, w, banks)
+        return op("v", lambda q: q.tensor_scalar(out, in0, s1, s2, op0, op1), r, w, banks)
+
+    def tt(out, in0, in1, o, r, w, banks=(), extra=()):
+        return op("v", lambda q: q.tensor_tensor(out, in0, in1, o), r, w, banks, extra)
+
+    def cp(out, in_, r, w, banks=()):
+        return op("v", lambda q: q.tensor_copy(out, in_), r, w, banks)
+
+    def act(out, in_, func, r, w, banks=(), bias=0.0, scale=1.0):
+        return op("a", lambda q: q.activation(out, in_, func, bias=bias, scale=scale), r, w, banks)
+
+    def mm(out, lhsT, rhs, start, stop, r, bk):
+        return op("p", lambda q: q.matmul(out, lhsT, rhs, start, stop), r, (), (bk,))
+
+    def iota(out, pat, base, cm, key, small=True):
+        if small:
+            return op("g", lambda q: q.iota(out, pat, base, cm, allow_small_or_imprecise_dtypes=True), (), (key,))
+        return op("g", lambda q: q.iota(out, pat, base, cm), (), (key,))
+
+    load("s", T.BR[:, 0:16], T.lo0[:], "lbr", 32, "BR")
+    load("a", T.BR[:, 16:32], T.hi0[:], "lbr", 32, "BR")
+    load("s", T.YT[:], T.ytab[:], "ly", 16, "YT")
+    load("a", T.HM[:], T.home[:], "lhm", 16, "HM")
+    load("s", T.X1[:, 0:256], T.xrow[:, 0:256], "lx0", 16, "X1_0a")
+    load("s", T.HI[:, 0:48], T.ha[:], "lhi", 32, "HI")
+    load("s", T.HI[:, 48:96], T.hb[:], "lhi", 32, "HI")
+    for l in range(1, 4):
+        for h in range(2):
+            load("s", T.X1[:, 512 * l + 256 * h:512 * l + 256 * h + 256], T.xrow[:, 256 * l:256 * l + 256], "lx1", 96,
+                 "X1_%d%s" % (l, "ab"[h]))
+
+    iota(T.PI[:], [[0, 4]], 0, 1, "PI", small=False)
+    iota(T.J[:], [[1, 144]], -15, 0, "J")
+    iota(T.EJ[:], [[1, 16], [0, 16]], 0, 0, "EJ")
+    iota(T.CJ[:], [[0, 16], [1, 16]], 0, 0, "CJ")
+    iota(T.J16[:], [[16, 8], [0, 16]], 0, 0, "J16")
+    op("v", lambda q: q.memset(T.LH[:], 0.0), (), ["LHl%d" % l for l in range(4)] + ["LHh%d" % l for l in range(4)] + ["LHm0", "LHm1"])
+    for k, (p0, p1, c, v) in enumerate(((0, 32, 0, 1.0), (0, 32, 1, -1 / 16), (32, 64, 0, 0.0), (32, 64, 1, 1 / 16), (64, 128, 0, -1.0), (64, 128, 1, 0.0))):
+        op("v", lambda q: q.memset(T.AB[p0:p1, c:c + 1], v), (), ("AB%d" % k,))
+    AB = ["AB%d" % k for k in range(6)]
+    for c, m in ((0, 127), (1, 31), (2, 112), (3, 15)):
+        ts(T.PJ[:, c:c + 1], T.PI[:, c:c + 1], m, None, A.bitwise_and, None, ("PI",), ("PJ%d" % c,))
+    cp(T.PC[:], T.PJ[:], ["PJ%d" % c for c in range(4)], ("PC",))
+    P, P31, GP, P15 = (T.PC[:, c:c + 1] for c in range(4))
+    JJ = T.J[:, 15:143]
+    ts(T.IH[:], JJ, P, None, A.is_equal, None, ("J", "PC"), ("IH",))
+    ts(T.EW[:], T.EJ[:], T.AB[:, 1:2], T.AB[:, 0:1], A.mult, A.add, ["EJ"] + AB, ("EW",))
+    ts(T.ED[:], T.CJ[:], P31, None, A.is_equal, None, ("CJ", "PC"), ("ED",))
+    tt(T.E[:], T.EW[:], T.ED[:], A.mult, ("EW", "ED"), ("E",))
+    ts(T.BR16[:], T.BR[:], -CEN, None, A.add, None, ("BR",), ("BR16",))
+    mm(T.PU[0:16, 0:128], T.BR16[:, 0:16], T.IH[:], True, True, ("BR16", "IH"), "PU")
+    mm(T.PV[0:16, 0:128], T.BR16[:, 16:32], T.IH[:], True, True, ("BR16", "IH"), "PV")
+    ts(T.HM16[:], T.HM[:], -CEN, None, A.add, None, ("HM",), ("HM16",))
+    for l in range(4):
+        mm(T.K1[0:16, 128 * l:128 * l + 128], T.HM16[:, 16 * l:16 * l + 16], T.IH[:], True, True, ("HM16", "IH"), "K1")
+    cp(T.LH[0:16, 0:128], T.PU[0:16, 0:128], (), ("LHl0",), ("PU",))
+    cp(T.LH[32:48, 0:128], T.PV[0:16, 0:128], (), ("LHh0",), ("PV",))
+    cp(T.LH[64:80, 0:128], T.K1[0:16, 0:128], (), ("LHm0",), ("K1",))
+
+    steps = [(s, l) for l in range(4) for s in range(2)]
+    YW = T.YT[:, 0:3072]
+    SHR, AND = A.logical_shift_right, A.bitwise_and
+
+    def piece(wd, i):
+        s, l = steps[i]
+        p = "0" if i < 2 else "%d" % ((i + 1) % 2)
+        d = "%d" % (i % 2)
+        OF, HF, JF, YG, D = T["OF" + p], T["HF" + p], T["JF" + p], T["YG" + p], T["D" + d]
+        lc = slice(128 * l, 128 * l + 128)
+        if s == 0:
+            x1, x2, xk = T.X1[:, 512 * l:512 * l + 256], T.X1[:, 512 * l:512 * l + 512], ("X1_%da" % l, "X1_%db" % l)
+        else:
+            x1, x2, xk = T.X2[:, 256 * l:256 * l + 256], None, ("X2_%d" % l,)
+        wk = "W%d%d" % (s, l)
+        k = int(wd[1:]) if wd[1:].isdigit() else None
+        if wd in ("ga", "gb"):
+            t = "ab".index(wd[1])
+            c0 = 768 * t + 256 * (l - 1)
+            win = T["W%d" % s][:, 0:48 * l].indirect(T.HO[:, 48 * t + 16 * (l - 1):48 * t + 16 * l])
+            tt(T["G" + "AB"[t]][:], win, T.MK[:, c0:c0 + 256], A.mult, ["HO", "MK%d" % (c0 // 512)] + ["W%d%d" % (s, j) for j in range(l)],
+               ("G%d" % t,), extra=[("d", "arr%d%d" % (s, l - 1), n_arr)])
+        elif wd in ("pu", "pv"):
+            t = "uv".index(wd[1])
+            nm = "P" + "UV"[t]
+            for q in range(16):
+                mm(T[nm][0:16, q:128:16], T["G" + "AB"[t]][:, q:256:16], T.BG[:], True, True, ("G%d" % t, "BG"), nm)
+        elif wd == "us":
+            act(T.US[0:16, :], T.PU[0:16, 0:128], F.Copy, (), ("US",), ("PU",))
+        elif wd == "ll":
+            tt(T.LH[0:16, lc], T.PV[0:16, 0:128], T.US[0:16, :], A.min, ("US",), ("LHl%d" % l,), ("PV",))
+        elif wd == "hh":
+            tt(T.LH[32:48, lc], T.PV[0:16, 0:128], T.US[0:16, :], A.max, ("US",), ("LHh%d" % l,), ("PV",))
+        elif wd == "ex":
+            ks = ("LHl%d" % l, "LHh%d" % l, "E")
+            mm(T.PZ[:, 0:256], T.LH[0:48, lc], T.E[0:48, :], True, True, ks, "PZ")
+            mm(T.PY[:, 0:256], T.LH[0:80, lc], T.E[0:80, :], True, True, ks + ("LHm%d" % min(l, 1),), "PY")
+        elif wd == "of":
+            ts(OF[:], T.PZ[:, 0:256], CEN - 15 / 32, None, A.add, None, (), ("OF" + p,), ("PZ",))
+        elif wd == "ha":
+            act(T.XZ[:], T.PY[:, 0:256], F.Abs, (), ("XZ",), ("PY",), bias=-15 / 512, scale=1 / 16)
+        elif wd == "hf":
+            ts(HF[:], T.XZ[:], -2047 - 15 / 32, None, A.add, None, ("XZ",), ("HF" + p,))
+        elif wd == "jf":
+            ts(JF[:], OF[:], -CEN, None, A.add, None, ("OF" + p,), ("JF" + p,))
+        elif wd[0] == "g":
+            act(YG[:, 512 * k:512 * k + 512], YW.indirect(OF[:, 32 * k:32 * k + 32]), F.Copy, ("YT", "OF" + p), ("YG%s%d" % (p, k),))
+        elif wd[0] == "p":
+            nm = "PD%d" % (k % 2)
+            mm(T[nm][:], T.IB[:], YG[:, 512 * k:512 * k + 512], True, False, ("IB", "YG%s%d" % (p, k)), nm)
+            if s == 0:
+                mm(T[nm][:], T.NI[:], x2, False, True, ("NI",) + xk, nm)
+            else:
+                mm(T[nm][:, 0:256], T.NI[:], x1, False, False, ("NI",) + xk, nm)
+                mm(T[nm][:, 256:512], T.NI[:], x1, False, True, ("NI",) + xk, nm)
+        elif wd[0] == "d":
+            if s == 0:
+                tt(D[:, 512 * k:512 * k + 512], YW.indirect(OF[:, 32 * k:32 * k + 32]), x2, A.subtract,
+                   ("YT", "OF" + p) + xk, ("D%s%da" % (d, k), "D%s%db" % (d, k)))
+            else:
+                for h in range(2):
+                    o = 512 * k + 256 * h
+                    tt(D[:, o:o + 256], YW.indirect(OF[:, o // 16:o // 16 + 16]), x1, A.subtract,
+                       ("YT", "OF" + p) + xk, ("D%s%d%s" % (d, k, "ab"[h]),))
+        elif wd[0] == "a" and k is not None:
+            Dk = D[:, 512 * k:512 * k + 512]
+            keys = ("D%s%da" % (d, k), "D%s%db" % (d, k))
+            if k < NBS[i]:
+                act(Dk, T["PD%d" % (k % 2)][:], F.Abs, (), keys, ("PD%d" % (k % 2),))
+            else:
+                act(Dk, Dk, F.Abs, keys, keys)
+        elif wd[0] == "q":
+            nm = "K%d" % (k % 2)
+            out = T[nm][:, 0:64]
+            keys = ["ZS"] + ["D%s%d%s" % (d, c, h) for c in (2 * k, 2 * k + 1) for h in "ab"]
+            mm(out, T.IK[:], HF[:, 64 * k:64 * k + 64], True, False, ("IK", "HF" + p), nm)
+            for q in range(16):
+                mm(out, T.ZS[:, 15 - q:143 - q], D[:, 1024 * k + q:1024 * k + 1024:16], False, False, keys, nm)
+            mm(out, T.IH[:], JF[:, 64 * k:64 * k + 64], False, True, ("IH", "JF" + p), nm)
+        elif wd == "ks":
+            act(T.R0[:], T.K0[:, 0:64], F.Copy, (), ("R0",), ("K0",))
+        elif wd[0] == "r":
+            nm = "K%d" % (k % 2)
+            tt(T["R%d" % k][:], T[nm][:, 0:64], T["R%d" % (k - 1)][:], A.min, ("R%d" % (k - 1),), ("R%d" % k,), (nm,))
+        elif wd == "w1":
+            tt(T.T3[:], T.R3[:, 0:32], T.R3[:, 32:64], A.min, ("R3",), ("T3",))
+        elif wd == "w2":
+            tt(T.T4[:], T.T3[:, 0:16], T.T3[:, 16:32], A.min, ("T3",), ("T4",))
+        elif wd == "w3":
+            ts(T.T5[:], T.T4[:], MAGIC, -MAGIC, A.add, A.add, ("T4",), ("T5",))
+        elif wd == "w4":
+            tok = tt(slot(T, s, l, 0), T.T4[:], T.T5[:], A.subtract, ("T4", "T5"), (wk,))
+            if l == 3:
+                return
+            need("g", [tok])
+            tr = []
+            for j in range(2):
+                first, dst, b = my_ways[j]
+                rid, pid = topo.addr(first, core)
+                tr.append(RemoteDMATransfer(dst_ids=[DstId(rid=rid, pnc=pid)], dma_engine_mask=bits(my_masks[j]),
+                                            remote_sem=T.sem["arr%d%d" % (s, l)], src=slot(T, s, l, 0), dst=slot(T, s, l, b)))
+            g.remote_dma_fused(tr, local_sem=T.sem.sent)
+        elif wd == "wo":
+            ts(T.WO[:], slot(T, s, l, 0), CEN, None, A.add, None, (wk,), ("WO",))
+        elif wd == "ld":
+            tt(T.LD[:], YW.indirect(T.WO[:, 0:16]), x1, A.subtract, ("YT", "WO", xk[0]), ("LD",))
+        elif wd == "la":
+            c = slice(256 * l, 256 * l + 256)
+            if s == 0:
+                act(T.X2[:, c], T.LD[:], F.Abs, ("LD",), ("X2_%d" % l,))
+            else:
+                act(T.XO[:, c], T.LD[:], F.Abs, ("LD",), ("XO%d" % l,))
+                store("s", T.xo[:, c], T.XO[:, c], ("XO%d" % l,))
+        elif wd == "ar":
+            act(T.AR[:, 64 * s + 16 * l:64 * s + 16 * l + 16], slot(T, s, l, 0), F.Identity, (wk,), ("AR%d%d" % (s, l),), bias=CEN)
+            if l == 3:
+                store("s" if s == 0 else "a", T.argm[:, 64 * s:64 * s + 64], T.AR[:, 64 * s:64 * s + 64], ["AR%d%d" % (s, j) for j in range(4)])
+        elif wd == "ib":
+            ts(T.IB[:], JJ, P, None, A.is_equal, None, ("J", "PC"), ("IB",))
+        elif wd == "ni":
+            ts(T.NI[:], JJ, P, -1.0, A.is_equal, A.mult, ("J", "PC"), ("NI",))
+        elif wd == "lm":
+            cp(T.LH[64:80, 128:512], T.K1[0:16, 128:512], (), ("LHm1",), ("K1",))
+        elif wd == "xb":
+            cp(T.X1[:, 256:512], T.X1[:, 0:256], ("X1_0a",), ("X1_0b",))
+        elif wd == "ik":
+            ts(T.IK[:], JJ, P, 4096.0, A.is_equal, A.mult, ("J", "PC"), ("IK",))
+        elif wd == "zs":
+            ts(T.ZS[:], T.J[:], GP, 4096.0, A.is_equal, A.mult, ("J", "PC"), ("ZS",))
+        elif wd == "h1":
+            ts(T.H4[:], T.HI[:], 15, None, AND, None, ("HI",), ("H4",))
+        elif wd == "h2":
+            ts(T.I16[:], T.J[:, 15:31], P15, None, A.is_equal, None, ("J", "PC"), ("I16",))
+        elif wd == "h3":
+            cp(T.HR[:], T.H4[:], ("H4",), ("HR",))
+        elif wd == "h4":
+            ts(T.H1[:], T.HI[:], 4, 15, SHR, AND, ("HI",), ("H1",))
+        elif wd == "h5":
+            ts(T.H2[:], T.HI[:], 8, None, SHR, None, ("HI",), ("H2",))
+        elif wd == "h6":
+            ts(T.H3[:], T.HI[:], 10, None, SHR, None, ("HI",), ("H3",))
+        elif wd == "h7":
+            ts(T.H2[:], T.H2[:], 48.0, None, A.mult, None, ("H2",), ("H2",))
+        elif wd == "h8":
+            ts(T.H3[:], T.H3[:], -176.0, None, A.mult, None, ("H3",), ("H3",))
+        elif wd == "h9":
+            tt(T.H1[:], T.H1[:], T.H2[:], A.add, ("H1", "H2"), ("H1",))
+        elif wd == "hA":
+            tt(T.H1[:], T.H1[:], T.H3[:], A.add, ("H1", "H3"), ("H1",))
+        elif wd == "hB":
+            cp(T.HO[:], T.H1[:], ("H1",), ("HO",))
+        elif wd == "hC":
+            ts(T.BO[:], T.J16[:], GP, None, A.is_equal, None, ("J16", "PC"), ("BO",))
+        elif wd == "hD":
+            ts(T.BG[:], T.J[:, 15:143:16], GP, None, A.is_equal, None, ("J", "PC"), ("BG",))
+        elif wd[0] == "s":
+            act(T.RD[:, k:1536:16], T.HR[:], F.Identity, ("HR", "I16"), ("RD%d" % k,), scale=T.I16[:, k:k + 1])
+        elif wd[0] == "m":
+            nm = ("PU", "PV", "PZ")[k]
+            mm(T[nm][:], T.BO[:], T.RD[:, 512 * k:512 * k + 512], True, True, ["BO"] + ["RD%d" % q for q in range(16)], nm)
+        elif wd[0] == "e":
+            nm = ("PU", "PV", "PZ")[k]
+            ts(T.MK[:, 512 * k:512 * k + 512], T[nm][:], P15, None, A.is_equal, None, ("PC",), ("MK%d" % k,), (nm,))
+        else:
+            raise ValueError(wd)
+
+    for word in ORDER.split():
+        wd, i = word.split(".")
+        piece(wd, int(i))
+
+    g.wait_ge(T.sem.sent, 6 * (len(my_masks[0]) + len(my_masks[1])))
+    for e in ("v", "a", "p", "g"):
+        g.wait_ge(T.sem[CS[e]], count[e])
+    g.wait_ge(T.sem.st, stores[0])

@@ -1,28 +1,19 @@
 from concourse.bass import DstId, RemoteDMATransfer
 from concourse.mybir import AluOpType as A, ActivationFunctionType as F
 
-NBS = [2, 2, 2, 2, 2, 2, 2, 2]
-ORDER = """
-lm.0 ex.0 of.0 ib.0 ha.0 zs.0 g0.0 hf.0 ni.0 g1.0 ik.0 xb.0 p0.0 jf.0 p1.0 a0.0 d3.0 d2.0 d4.0 d5.0 d6.0 a3.0 a1.0 q0.0
-d7.0 a2.0 a4.0 h1.0 ks.0 q1.0 h2.0 a5.0 r1.0 h6.0 q2.0 a6.0 h3.0 a7.0 h5.0 s9.0 s0.0 r2.0 s12.0 h7.0 s11.0 h4.0 s3.0
-s13.0 s15.0 hC.0 s10.0 h9.0 q3.0 r3.0 w1.0 w2.0 s7.0 w3.0 s1.0 s14.0 w4.0 wo.0 s2.0 h8.0 ld.0 s5.0 la.0 s8.0
-p1.1 s6.0 hA.0 a1.1 s4.0 hD.0 hB.0 d6.1 d5.1 a6.1 p0.1 d3.1 m1.0 m2.0 d2.1 d4.1 a0.1 m0.0 q0.1 e0.0 a5.1 d7.1 e2.0
-a3.1 a2.1 q1.1 ks.1 r1.1 a4.1 q2.1 e1.0 a7.1 r2.1 q3.1 ga.2 gb.2 r3.1 w1.1 pu.2 pv.2 us.2 w2.1 ll.2 ar.0 hh.2 w3.1 w4.1
-ex.2 of.2 ha.2 g0.2 wo.1 g1.2 d2.2 p0.2 d3.2 d4.2 p1.2 hf.2 a2.2 jf.2 a0.2 a1.2 d5.2 a3.2 a4.2 a5.2 d6.2 d7.2 q0.2
-ga.3 ks.2 gb.3 q1.2 q2.2 r1.2 ld.1 a6.2 pu.3 a7.2 r2.2 us.3 pv.3 ll.3 hh.3 q3.2 r3.2 la.1 w1.2 ex.3 w2.2 w3.2 w4.2 wo.2
-ld.2 ha.3 of.3 hf.3 la.2 jf.3 g0.3 p0.3 g1.3 d2.3 d4.3 a2.3 d3.3 a0.3 p1.3 d5.3 d6.3 a1.3 a3.3 d7.3 q0.3 q1.3 a4.3
-ks.3 a5.3 a6.3 q2.3 a7.3 ga.4 pu.4 r1.3 us.4 q3.3 gb.4 r2.3 r3.3 w1.3 pv.4 ll.4 hh.4 w2.3 w3.3 w4.3 ex.4 of.4 ha.4
-g0.4 g1.4 p0.4 wo.3 p1.4 d2.4 d4.4 jf.4 hf.4 d3.4 d5.4 a2.4 a0.4 d6.4 a1.4 a3.4 q0.4 q1.4 a4.4 ks.4 d7.4 r1.4 a5.4
-ld.3 q2.4 r2.4 a6.4 a7.4 q3.4 ga.5 gb.5 r3.4 w1.4 w2.4 pu.5 pv.5 w3.4 la.3 us.5 ll.5 w4.4 hh.5 ex.5 wo.4 ld.4 ha.5
-of.5 la.4 g0.5 hf.5 g1.5 jf.5 d2.5 p0.5 a2.5 d3.5 p1.5 a0.5 d4.5 d5.5 d6.5 a1.5 q0.5 a3.5 a4.5 a5.5 d7.5 ks.5 ga.6
-q1.5 q2.5 a6.5 r1.5 r2.5 pu.6 a7.5 gb.6 q3.5 r3.5 us.6 pv.6 ar.2 w1.5 ll.6 hh.6 w2.5 w3.5 ex.6 w4.5 of.6 wo.5 ha.6
-jf.6 g0.6 p0.6 d3.6 d4.6 d2.6 g1.6 a3.6 a0.6 p1.6 a1.6 hf.6 d5.6 d6.6 a2.6 a5.6 d7.6 q0.6 q1.6 a4.6 ks.6 a6.6 r1.6
-a7.6 q2.6 ld.5 r2.6 ga.7 q3.6 ar.4 gb.7 pu.7 pv.7 us.7 r3.6 la.5 w1.6 w2.6 w3.6 ll.7 hh.7 w4.6 ar.3 ex.7 ar.5 wo.6
-ar.6 ld.6 ha.7 of.7 hf.7 la.6 jf.7 g0.7 g1.7 d2.7 p0.7 d3.7 d5.7 a2.7 d4.7 d6.7 p1.7 a0.7 a1.7 a3.7 q0.7 a4.7 ks.7
-d7.7 a5.7 a6.7 q1.7 r1.7 a7.7 ar.1 q2.7 q3.7 r2.7 r3.7 w1.7 w2.7 w3.7 w4.7 ar.7 wo.7 ld.7 la.7
+KINDS = ["BBCCBBCC"] * 8
+COPY = "aa"
+HFON = "a"
+CYCLE = """
+a6.1 c0.1 mb.2 lh.2 s103.1 ez.2 of.2 c1.1 k1.1 k2.1 sc.1 w3.1 g3.2 g2.2 hm.2 w4.1 p3.2 d5.2 z1.2 wo.1 d4.2 ey.2 g6.2 p2.2
+p6.2 ha.2 g7.2 zu.3 hf.2 d1.2 t102.2 k0.2 d0.2 r5.2 r4.2 r0.2 r1.2 a2.2 a3.2 z0.2 a6.2 ld.1 t002.2 p7.2 ga.3 a7.2 s004.2
+hi.3 ky.4 gb.3 s103.2 c0.2 la.1 ma.3 s13.2 mb.3 k1.2 c1.2 lh.3 k2.2 ey.3 sc.2 ez.3 e1.4 ha.3 m2.3 z0.3 w3.2 of.3 z1.3
+w4.2 g2.3 wo.2 ld.2 la.2 p2.3 d1.3 g6.3 d0.3 d4.3 p6.3 t002.3 hf.3 r1.3 sg.4 g3.3 g7.3 d5.3 p3.3 r0.3 m1.3 a2.3 r4.3
+k0.3 p7.3 t102.3 zu.4 a3.3 ga.4 m3.3 s004.3 ma.4 gb.4 r5.3 a7.3 s13.3
 """
 CEN = 1536.0
 MAGIC = 1.5 * 2.0 ** 35
+WHOLE = 1.5 * 2.0 ** 23
 
 
 def _sb(n, d):
@@ -32,24 +23,23 @@ def _sb(n, d):
 SCRATCH = {
     "YT": _sb(3072, "bfloat16"), "X1": _sb(2048, "bfloat16"), "X2": _sb(1024, "bfloat16"),
     "XO": _sb(1024, "float32"), "AR": _sb(128, "float32"),
-    "D0": _sb(4096, "bfloat16"), "D1": _sb(4096, "bfloat16"), "YG0": _sb(1536, "bfloat16"), "YG1": _sb(1536, "bfloat16"),
-    "OF0": _sb(256, "uint16"), "OF1": _sb(256, "uint16"), "JF0": _sb(256, "float16"), "JF1": _sb(256, "float16"),
+    "D0": _sb(4096, "bfloat16"), "D1": _sb(4096, "bfloat16"), "Y0": _sb(4096, "bfloat16"), "Y1": _sb(4096, "bfloat16"),
+    "OF0": _sb(256, "uint16"), "OF1": _sb(256, "uint16"),
     "HF0": _sb(256, "float16"), "HF1": _sb(256, "float16"), "XZ": _sb(256, "float32"),
-    "W0": _sb(192, "float32"), "W1": _sb(192, "float32"), "GA": _sb(256, "float16"), "GB": _sb(256, "float16"),
-    "US": _sb(128, "float32"), "LH": _sb(512, "float16"),
-    "R0": _sb(64, "float32"), "R1": _sb(64, "float32"), "R2": _sb(64, "float32"), "R3": _sb(64, "float32"),
-    "T3": _sb(32, "float32"), "T4": _sb(16, "float32"), "T5": _sb(16, "float32"),
-    "WO": _sb(16, "uint16"), "LD": _sb(256, "bfloat16"),
-    "BR": _sb(32, "int32"), "BR16": _sb(32, "float16"), "HM": _sb(64, "int32"), "HM16": _sb(64, "float16"),
-    "HI": _sb(96, "int32"), "H1": _sb(96, "int32"), "H2": _sb(96, "int32"), "H3": _sb(96, "int32"), "H4": _sb(96, "int32"),
-    "HO": _sb(96, "uint16"), "HR": _sb(96, "float32"), "RD": _sb(1536, "bfloat16"), "MK": _sb(1536, "bfloat16"),
-    "PI": _sb(4, "int32"), "PJ": _sb(4, "int32"), "PC": _sb(4, "float32"), "AB": _sb(2, "float32"),
-    "J": _sb(144, "float32"), "J16": _sb(128, "float32"), "CJ": _sb(256, "float32"), "EJ": _sb(256, "float32"),
-    "EW": _sb(256, "float16"), "ED": _sb(256, "float16"), "E": _sb(256, "float16"),
+    "W0": _sb(192, "float32"), "W1": _sb(192, "float32"), "G": _sb(512, "float16"), "LH": _sb(512, "float16"),
+    "S0": _sb(128, "float16"), "S1": _sb(128, "float16"), "KS": _sb(256, "float32"), "T5": _sb(16, "float32"),
+    "WO": _sb(128, "uint16"), "LD": _sb(256, "bfloat16"),
+    "BR": _sb(32, "int32"), "BR16": _sb(48, "float16"), "HM": _sb(64, "int32"), "HM16": _sb(64, "float16"),
+    "HI": _sb(96, "int32"), "H1": _sb(96, "int32"), "H2": _sb(96, "int32"), "H3": _sb(96, "int32"), "HX": _sb(192, "int32"),
+    "HO": _sb(192, "uint16"), "MK": _sb(1536, "bfloat16"),
+    "PI": _sb(4, "int32"), "PC": _sb(4, "float32"), "AB": _sb(8, "float32"),
+    "J": _sb(128, "bfloat16"), "JP": _sb(128, "bfloat16"), "EJ": _sb(512, "bfloat16"), "CJ": _sb(256, "bfloat16"),
+    "EW": _sb(512, "float16"), "ED": _sb(512, "float16"), "E": _sb(512, "float16"),
     "IH": _sb(128, "float16"), "IK": _sb(128, "float16"), "IB": _sb(128, "bfloat16"), "NI": _sb(128, "bfloat16"),
-    "BO": _sb(128, "bfloat16"), "ZS": _sb(144, "bfloat16"), "BG": _sb(8, "float16"), "I16": _sb(16, "float32"),
+    "PM": _sb(128, "float16"), "BH": _sb(16, "float16"), "BB": _sb(16, "bfloat16"), "I16": _sb(16, "bfloat16"),
+    "ZZ": _sb(128, "bfloat16"), "RS": _sb(256, "bfloat16"), "ON": _sb(128, "bfloat16"), "MM": _sb(512, "bfloat16"),
 }
-for _n in ("K0", "K1", "PU", "PV", "PZ", "PY", "PD0", "PD1"):
+for _n in ("P0", "P1", "K", "PU", "PZ", "PD0", "PD1", "PD2"):
     SCRATCH[_n] = ("psum", [128, 512], "float32")
 SEMAPHORES = ["cv", "ca", "cp", "cg", "lbr", "lhm", "ly", "lx0", "lhi", "lx1", "st", "sent"] + \
              ["arr%d%d" % (s, l) for s in range(2) for l in range(3)]
@@ -105,6 +95,11 @@ def relay_program(g, core, T, topo, src, ways, k):
             g.wait_ge(sem, n_in)
             g.remote_dma(slot(T, s, l, b), slot(T, s, l, b), sem, T.sem.sent, pid, rid, topo.mask(core, dst))
     g.wait_ge(T.sem.sent, 6 * n_out)
+
+
+def order():
+    words = [wd.split(".") for wd in CYCLE.split()]
+    return [(wd, n + int(j)) for n in range(-6, 14, 2) for wd, j in words if 0 <= n + int(j) < 8]
 
 
 def rank_program(g, core, T, topo):
@@ -193,11 +188,14 @@ def rank_program(g, core, T, topo):
     def cp(out, in_, r, w, banks=()):
         return op("v", lambda q: q.tensor_copy(out, in_), r, w, banks)
 
+    def fill(out, v, w, r=()):
+        return op("v", lambda q: q.memset(out, v), r, w)
+
     def act(out, in_, func, r, w, banks=(), bias=0.0, scale=1.0):
         return op("a", lambda q: q.activation(out, in_, func, bias=bias, scale=scale), r, w, banks)
 
-    def mm(out, lhsT, rhs, start, stop, r, bk):
-        return op("p", lambda q: q.matmul(out, lhsT, rhs, start, stop), r, (), (bk,))
+    def mm(out, lhsT, rhs, start, stop, r, bk, w=()):
+        return op("p", lambda q: q.matmul(out, lhsT, rhs, start, stop), r, w, (bk,))
 
     def iota(out, pat, base, cm, key, small=True):
         if small:
@@ -206,136 +204,204 @@ def rank_program(g, core, T, topo):
 
     load("s", T.BR[:, 0:16], T.lo0[:], "lbr", 32, "BR")
     load("a", T.BR[:, 16:32], T.hi0[:], "lbr", 32, "BR")
+    load("a", T.X1[:, 0:256], T.xrow[:, 0:256], "lx0", 16, "X0")
     load("s", T.YT[:], T.ytab[:], "ly", 16, "YT")
     load("a", T.HM[:], T.home[:], "lhm", 16, "HM")
-    load("s", T.X1[:, 0:256], T.xrow[:, 0:256], "lx0", 16, "X1_0a")
-    load("s", T.HI[:, 0:48], T.ha[:], "lhi", 32, "HI")
-    load("s", T.HI[:, 48:96], T.hb[:], "lhi", 32, "HI")
+    for l in range(3):
+        for t, src in enumerate((T.ha, T.hb)):
+            load("s", T.HI[:, 32 * l + 16 * t:32 * l + 16 * t + 16], src[:, 16 * l:16 * l + 16], "lhi", 96, "HI")
     for l in range(1, 4):
         for h in range(2):
             load("s", T.X1[:, 512 * l + 256 * h:512 * l + 256 * h + 256], T.xrow[:, 256 * l:256 * l + 256], "lx1", 96,
-                 "X1_%d%s" % (l, "ab"[h]))
+                 "X1_%d" % l)
 
+    SHR, AND = A.logical_shift_right, A.bitwise_and
     iota(T.PI[:], [[0, 4]], 0, 1, "PI", small=False)
-    iota(T.J[:], [[1, 144]], -15, 0, "J")
-    iota(T.EJ[:], [[1, 16], [0, 16]], 0, 0, "EJ")
-    iota(T.CJ[:], [[0, 16], [1, 16]], 0, 0, "CJ")
-    iota(T.J16[:], [[16, 8], [0, 16]], 0, 0, "J16")
-    op("v", lambda q: q.memset(T.LH[:], 0.0), (), ["LHl%d" % l for l in range(4)] + ["LHh%d" % l for l in range(4)] + ["LHm0", "LHm1"])
-    for k, (p0, p1, c, v) in enumerate(((0, 32, 0, 1.0), (0, 32, 1, -1 / 16), (32, 64, 0, 0.0), (32, 64, 1, 1 / 16), (64, 128, 0, -1.0), (64, 128, 1, 0.0))):
-        op("v", lambda q: q.memset(T.AB[p0:p1, c:c + 1], v), (), ("AB%d" % k,))
-    AB = ["AB%d" % k for k in range(6)]
-    for c, m in ((0, 127), (1, 31), (2, 112), (3, 15)):
-        ts(T.PJ[:, c:c + 1], T.PI[:, c:c + 1], m, None, A.bitwise_and, None, ("PI",), ("PJ%d" % c,))
-    cp(T.PC[:], T.PJ[:], ["PJ%d" % c for c in range(4)], ("PC",))
-    P, P31, GP, P15 = (T.PC[:, c:c + 1] for c in range(4))
-    JJ = T.J[:, 15:143]
-    ts(T.IH[:], JJ, P, None, A.is_equal, None, ("J", "PC"), ("IH",))
-    ts(T.EW[:], T.EJ[:], T.AB[:, 1:2], T.AB[:, 0:1], A.mult, A.add, ["EJ"] + AB, ("EW",))
-    ts(T.ED[:], T.CJ[:], P31, None, A.is_equal, None, ("CJ", "PC"), ("ED",))
-    tt(T.E[:], T.EW[:], T.ED[:], A.mult, ("EW", "ED"), ("E",))
-    ts(T.BR16[:], T.BR[:], -CEN, None, A.add, None, ("BR",), ("BR16",))
-    mm(T.PU[0:16, 0:128], T.BR16[:, 0:16], T.IH[:], True, True, ("BR16", "IH"), "PU")
-    mm(T.PV[0:16, 0:128], T.BR16[:, 16:32], T.IH[:], True, True, ("BR16", "IH"), "PV")
-    ts(T.HM16[:], T.HM[:], -CEN, None, A.add, None, ("HM",), ("HM16",))
-    for l in range(4):
-        mm(T.K1[0:16, 128 * l:128 * l + 128], T.HM16[:, 16 * l:16 * l + 16], T.IH[:], True, True, ("HM16", "IH"), "K1")
-    cp(T.LH[0:16, 0:128], T.PU[0:16, 0:128], (), ("LHl0",), ("PU",))
-    cp(T.LH[32:48, 0:128], T.PV[0:16, 0:128], (), ("LHh0",), ("PV",))
-    cp(T.LH[64:80, 0:128], T.K1[0:16, 0:128], (), ("LHm0",), ("K1",))
+    iota(T.J[:], [[1, 128]], 0, 0, "J")
+    iota(T.EJ[:, 256:512], [[0, 16], [1, 16]], 0, 0, "EJ1")
+    iota(T.EJ[:, 0:256], [[1, 2], [2, 8], [0, 16]], 0, 0, "EJ0")
+    iota(T.CJ[:], [[1, 16], [0, 16]], 0, 0, "CJ")
+    iota(T.JP[:], [[1, 16], [16, 8]], 0, 0, "JP")
+    LHK = ["LH%d" % l for l in range(4)]
+    fill(T.AB[:], 0.0, ("AB",))
+    fill(T.LH[:], 0.0, LHK + ["LHm"])
+    for c, m in ((1, 16), (2, 112), (3, 15)):
+        ts(T.PI[:, c:c + 1], T.PI[:, 0:1], m, None, AND, None, ("PI",), ("PI%d" % c,))
+    AB = ["AB%d" % k for k in range(11)]
+    for k, (p0, p1, c, v) in enumerate(((64, 96, 1, -15 / 32), (32, 64, 0, 1 / 8), (32, 64, 1, -1.0), (96, 128, 1, -1.0), (64, 96, 2, 1.0),
+                                        (0, 32, 3, -4096.0), (32, 64, 4, -CEN), (64, 65, 0, CEN / 8), (64, 65, 1, -CEN))):
+        fill(T.AB[p0:p1, c:c + 1], v, (AB[k],), ("AB", "AB0") if k == 8 else ("AB",))
+        if k == 4:
+            cp(T.PC[:], T.PI[:], ("PI", "PI1", "PI2", "PI3"), ("PC",))
+    P, GP, P15 = T.PC[:, 0:1], T.PC[:, 2:3], T.PC[:, 3:4]
+    ts(T.AB[0:32, 0:1], T.PC[0:32, 1:2], 1 / 128, -1 / 16, A.mult, A.add, ("PC", "AB"), (AB[9],))
+    ts(T.AB[0:32, 1:2], T.PC[0:32, 1:2], -1 / 16, 1.0, A.mult, A.add, ("PC", "AB"), (AB[10],))
+    ts(T.IH[:], T.J[:], P, None, A.is_equal, None, ("J", "PC"), ("IH",))
+    fill(T.LH[64:66, :], 1.0, LHK)
+    fill(T.BR16[:, 32:48], 0.0, ("BR0",))
+
+    def weights(h):
+        c = slice(256 * h, 256 * h + 256)
+        act(T.EW[:, c], T.EJ[:, c], F.Identity, ["EJ%d" % h] + AB, ("EW%d" % h,), bias=T.AB[:, 1:2], scale=T.AB[:, 0:1])
+        ts(T.ED[:, c], (T.EJ[:, 256:512], T.CJ[:])[h], P15, T.AB[:, 2:3], A.is_equal, A.max, [("EJ1", "CJ")[h], "PC"] + AB, ("ED%d" % h,))
+        tt(T.E[:, c], T.EW[:, c], T.ED[:, c], A.mult, ("EW%d" % h, "ED%d" % h), ("E%d" % h,))
+
+    weights(0)
+    ts(T.BR16[:, 0:32], T.BR[:], -CEN, None, A.add, None, ("BR",), ("BR16",))
+    mm(T.PU[0:48, 0:128], T.BR16[:], T.IH[:], True, True, ("BR16", "BR0", "IH"), "PU")
+
+    def homes():
+        ts(T.HM16[:], T.HM[:], -CEN, None, A.add, None, ("HM",), ("HM16",))
+        for l in range(4):
+            mm(T.K[0:16, 128 * l:128 * l + 128], T.HM16[:, 16 * l:16 * l + 16], T.IH[:], True, True, ("HM16", "IH"), "K")
+        act(T.LH[96:112, :], T.K[0:16, :], F.Copy, (), ("LHm",), ("K",))
+
+    def signs():
+        ts(T.IB[:], T.J[:], P, None, A.is_equal, None, ("J", "PC"), ("IB",))
+        act(T.NI[:], T.IH[:], F.Copy, ("IH",), ("NI",), scale=-1.0)
+        fill(T.ZZ[:], 0.0, ("ZZ",))
+        cp(T.X1[:, 256:512], T.X1[:, 0:256], ("X0",), ("X1_0",))
+        for t in range(2):
+            ts(T.BB[:, 8 * t:8 * t + 8], T.J[:, 0:128:16], GP, 1.0 - 2 * t, A.is_equal, A.mult, ("J", "PC"), ("BB%d" % t,))
+
+    def keyed():
+        act(T.IK[:], T.IH[:], F.Copy, ("IH",), ("IK",), scale=4096.0)
+        ts(T.PM[:], T.JP[:], P, 4096.0, A.is_equal, A.mult, ("JP", "PC"), ("PM",))
+        ts(T.RS[:], T.EJ[:, 256:512], 0.0, 2.0 ** 25, A.is_equal, A.mult, ("EJ1",), ("RS",))
+        fill(T.ON[0:1, :], 1.0, ("ON",))
+        fill(T.MM[0:1, 0:256], WHOLE, ("MM0",))
+        fill(T.MM[0:1, 256:512], -WHOLE, ("MM1",))
+
+    def hints():
+        ts(T.H1[:], T.HI[:], 2, 192, SHR, AND, ("HI",), ("H1",))
+        ts(T.H2[:], T.HI[:], 6, 48, SHR, AND, ("HI",), ("H2",))
+        ts(T.H3[:], T.HI[:], 4, 15, SHR, AND, ("HI",), ("H3",))
+        ts(T.HX[:, 96:192], T.HI[:], 15, None, AND, None, ("HI",), ("HQ",))
+        ts(T.H1[:], T.H1[:], 0.75, None, A.mult, None, ("H1",), ("H1",))
+        tt(T.H2[:], T.H2[:], T.H3[:], A.add, ("H2", "H3"), ("H2",))
+        ts(T.I16[:], T.J[:, 0:16], P15, None, A.is_equal, None, ("J", "PC"), ("I16",))
+        tt(T.HX[:, 0:96], T.H1[:], T.H2[:], A.add, ("H1", "H2"), ("HX",))
+        act(T.BH[:], T.BB[:], F.Copy, ("BB0", "BB1"), ("BH",))
+        cp(T.HO[:], T.HX[:], ("HX", "HQ"), ("HO",))
+
+    def mask(l):
+        act(T.MK[:, 512 * l - 512:512 * l], T.I16[:, 0:16].indirect(T.HO[:, 64 + 32 * l:96 + 32 * l]), F.Copy, ("I16", "HO"), ("MK%d" % l,))
 
     steps = [(s, l) for l in range(4) for s in range(2)]
     YW = T.YT[:, 0:3072]
-    SHR, AND = A.logical_shift_right, A.bitwise_and
+    pieces = order()
+    pd = [(i, k) for i in range(8) for k in range(8) if KINDS[i][k] == "C"]
+    pd = {c: "PD%d" % (n % 3) for n, c in enumerate(pd)}
+    once = {"e1": (0, lambda: weights(1)), "hm": (0, homes), "sg": (0, signs), "ky": (0, keyed), "hi": (1, hints),
+            "m1": (1, lambda: mask(1)), "m2": (1, lambda: mask(2)), "m3": (1, lambda: mask(3))}
 
     def piece(wd, i):
         s, l = steps[i]
         p = "0" if i < 2 else "%d" % ((i + 1) % 2)
         d = "%d" % (i % 2)
-        OF, HF, JF, YG, D = T["OF" + p], T["HF" + p], T["JF" + p], T["YG" + p], T["D" + d]
+        OF, HF, Y, D = T["OF" + p], T["HF" + p], T["Y" + p], T["D" + d]
         lc = slice(128 * l, 128 * l + 128)
         if s == 0:
-            x1, x2, xk = T.X1[:, 512 * l:512 * l + 256], T.X1[:, 512 * l:512 * l + 512], ("X1_%da" % l, "X1_%db" % l)
+            x1, x2, xk = T.X1[:, 512 * l:512 * l + 256], T.X1[:, 512 * l:512 * l + 512], "X1_%d" % l
         else:
-            x1, x2, xk = T.X2[:, 256 * l:256 * l + 256], None, ("X2_%d" % l,)
+            x1, x2, xk = T.X2[:, 256 * l:256 * l + 256], None, "X2_%d" % l
         wk = "W%d%d" % (s, l)
-        k = int(wd[1:]) if wd[1:].isdigit() else None
-        if wd in ("ga", "gb"):
+        wo = slice(64 * s + 16 * l, 64 * s + 16 * l + 16)
+        if wd in once:
+            if i == once[wd][0]:
+                once[wd][1]()
+            return
+        k = int(wd[1]) if wd[1].isdigit() else None
+        kind = KINDS[i][k] if wd[0] in "gpadr" and k is not None else None
+        if i < 2 and wd in ("zu", "ga", "gb", "ma", "mb") or \
+                i == 1 and (wd in ("lh", "ez", "ey", "of", "ha", "hf") or wd[0] == "g" and KINDS[0][k] == "C"):
+            return
+        if kind is not None:
+            k1 = int(wd[-1]) + 1
+            ck = slice(512 * k, 512 * k1)
+            yk, dk = (tuple("%s%d%s" % (nm, j, h) for j in range(k, k1) for h in "ab") for nm in ("Y" + p, "D" + d))
+        if wd == "zu":
+            mm(T.PU[0:48, 0:128], T.ZZ[0:32, 0:48], T.ZZ[0:32, :], True, False, ("ZZ",), "PU")
+        elif wd in ("ga", "gb"):
             t = "ab".index(wd[1])
-            c0 = 768 * t + 256 * (l - 1)
-            win = T["W%d" % s][:, 0:48 * l].indirect(T.HO[:, 48 * t + 16 * (l - 1):48 * t + 16 * l])
-            tt(T["G" + "AB"[t]][:], win, T.MK[:, c0:c0 + 256], A.mult, ["HO", "MK%d" % (c0 // 512)] + ["W%d%d" % (s, j) for j in range(l)],
+            c0 = 512 * (l - 1) + 256 * t
+            win = T["W%d" % s][:, 0:48 * l].indirect(T.HO[:, c0 // 16:c0 // 16 + 16])
+            tt(T.G[:, 256 * t:256 * t + 256], win, T.MK[:, c0:c0 + 256], A.mult, ["HO", "MK%d" % l] + ["W%d%d" % (s, j) for j in range(l)],
                ("G%d" % t,), extra=[("d", "arr%d%d" % (s, l - 1), n_arr)])
-        elif wd in ("pu", "pv"):
-            t = "uv".index(wd[1])
-            nm = "P" + "UV"[t]
+        elif wd == "ma":
             for q in range(16):
-                mm(T[nm][0:16, q:128:16], T["G" + "AB"[t]][:, q:256:16], T.BG[:], True, True, ("G%d" % t, "BG"), nm)
-        elif wd == "us":
-            act(T.US[0:16, :], T.PU[0:16, 0:128], F.Copy, (), ("US",), ("PU",))
-        elif wd == "ll":
-            tt(T.LH[0:16, lc], T.PV[0:16, 0:128], T.US[0:16, :], A.min, ("US",), ("LHl%d" % l,), ("PV",))
-        elif wd == "hh":
-            tt(T.LH[32:48, lc], T.PV[0:16, 0:128], T.US[0:16, :], A.max, ("US",), ("LHh%d" % l,), ("PV",))
-        elif wd == "ex":
-            ks = ("LHl%d" % l, "LHh%d" % l, "E")
-            mm(T.PZ[:, 0:256], T.LH[0:48, lc], T.E[0:48, :], True, True, ks, "PZ")
-            mm(T.PY[:, 0:256], T.LH[0:80, lc], T.E[0:80, :], True, True, ks + ("LHm%d" % min(l, 1),), "PY")
+                mm(T.PU[32:48, q:128:16], T.G[:, q:256:16], T.BH[:, 0:8], False, False, ("G0", "BH"), "PU")
+        elif wd == "mb":
+            for q in range(16):
+                mm(T.PU[32:48, q:128:16], T.G[:, 256 + q:512:16], T.BH[:, 8:16], False, q == 15, ("G1", "BH"), "PU")
+                mm(T.PU[0:32, q:128:16], T.G[:, q:512:16], T.BH[:, 0:8], False, q == 15, ("G0", "G1", "BH"), "PU")
+        elif wd == "lh":
+            ts(T.LH[0:48, lc], T.PU[0:48, 0:128], T.AB[0:48, 3:4], T.AB[0:48, 4:5], A.max, A.add, AB, ("LH%d" % l,), ("PU",))
+        elif wd == "ez":
+            mm(T.PZ[:, 0:256], T.LH[0:66, lc], T.E[0:66, 0:256], True, True, ("LH%d" % l, "E0"), "PZ")
+        elif wd == "ey":
+            mm(T.PU[:, 128:384], T.LH[0:112, lc], T.E[0:112, 256:512], True, True, ("LH%d" % l, "LHm", "E1"), "PU")
         elif wd == "of":
-            ts(OF[:], T.PZ[:, 0:256], CEN - 15 / 32, None, A.add, None, (), ("OF" + p,), ("PZ",))
+            ts(OF[:], T.PZ[:, 0:256], CEN, None, A.add, None, (), ("OF" + p,), ("PZ",))
         elif wd == "ha":
-            act(T.XZ[:], T.PY[:, 0:256], F.Abs, (), ("XZ",), ("PY",), bias=-15 / 512, scale=1 / 16)
+            act(T.XZ[:], T.PU[:, 128:384], F.Abs, (), ("XZ",), ("PU",), scale=1 / 16)
         elif wd == "hf":
-            ts(HF[:], T.XZ[:], -2047 - 15 / 32, None, A.add, None, ("XZ",), ("HF" + p,))
-        elif wd == "jf":
-            ts(JF[:], OF[:], -CEN, None, A.add, None, ("OF" + p,), ("JF" + p,))
-        elif wd[0] == "g":
-            act(YG[:, 512 * k:512 * k + 512], YW.indirect(OF[:, 32 * k:32 * k + 32]), F.Copy, ("YT", "OF" + p), ("YG%s%d" % (p, k),))
-        elif wd[0] == "p":
-            nm = "PD%d" % (k % 2)
-            mm(T[nm][:], T.IB[:], YG[:, 512 * k:512 * k + 512], True, False, ("IB", "YG%s%d" % (p, k)), nm)
-            if s == 0:
-                mm(T[nm][:], T.NI[:], x2, False, True, ("NI",) + xk, nm)
+            if HFON == "a":
+                act(HF[:], T.XZ[:], F.Identity, ("XZ",), ("HF" + p,), bias=-2047 - 15 / 32)
             else:
-                mm(T[nm][:, 0:256], T.NI[:], x1, False, False, ("NI",) + xk, nm)
-                mm(T[nm][:, 256:512], T.NI[:], x1, False, True, ("NI",) + xk, nm)
+                ts(HF[:], T.XZ[:], -2047 - 15 / 32, None, A.add, None, ("XZ",), ("HF" + p,))
+        elif wd[0] == "g":
+            act(Y[:, ck], YW.indirect(OF[:, 32 * k:32 * k1]), F.Copy, ("YT", "OF" + p), yk)
+        elif wd[0] == "p":
+            nm = pd[i, k]
+            mm(T[nm][:], T.IB[:], Y[:, ck], True, False, ("IB",) + yk, nm)
+            if s == 0:
+                mm(T[nm][:], T.NI[:], x2, False, True, ("NI", xk), nm)
+            else:
+                mm(T[nm][:, 0:256], T.NI[:], x1, False, False, ("NI", xk), nm)
+                mm(T[nm][:, 256:512], T.NI[:], x1, False, True, ("NI", xk), nm)
+        elif wd[0] == "a":
+            if kind == "C":
+                act(D[:, ck], T[pd[i, k]][:], F.Abs, (), dk, (pd[i, k],))
+            else:
+                act(D[:, ck], Y[:, ck], F.Abs, yk, dk)
         elif wd[0] == "d":
             if s == 0:
-                tt(D[:, 512 * k:512 * k + 512], YW.indirect(OF[:, 32 * k:32 * k + 32]), x2, A.subtract,
-                   ("YT", "OF" + p) + xk, ("D%s%da" % (d, k), "D%s%db" % (d, k)))
+                tt(Y[:, ck], YW.indirect(OF[:, 32 * k:32 * k + 32]), x2, A.subtract, ("YT", "OF" + p, xk), yk)
             else:
                 for h in range(2):
                     o = 512 * k + 256 * h
-                    tt(D[:, o:o + 256], YW.indirect(OF[:, o // 16:o // 16 + 16]), x1, A.subtract,
-                       ("YT", "OF" + p) + xk, ("D%s%d%s" % (d, k, "ab"[h]),))
-        elif wd[0] == "a" and k is not None:
-            Dk = D[:, 512 * k:512 * k + 512]
-            keys = ("D%s%da" % (d, k), "D%s%db" % (d, k))
-            if k < NBS[i]:
-                act(Dk, T["PD%d" % (k % 2)][:], F.Abs, (), keys, ("PD%d" % (k % 2),))
-            else:
-                act(Dk, Dk, F.Abs, keys, keys)
-        elif wd[0] == "q":
-            nm = "K%d" % (k % 2)
-            out = T[nm][:, 0:64]
-            keys = ["ZS"] + ["D%s%d%s" % (d, c, h) for c in (2 * k, 2 * k + 1) for h in "ab"]
-            mm(out, T.IK[:], HF[:, 64 * k:64 * k + 64], True, False, ("IK", "HF" + p), nm)
-            for q in range(16):
-                mm(out, T.ZS[:, 15 - q:143 - q], D[:, 1024 * k + q:1024 * k + 1024:16], False, False, keys, nm)
-            mm(out, T.IH[:], JF[:, 64 * k:64 * k + 64], False, True, ("IH", "JF" + p), nm)
-        elif wd == "ks":
-            act(T.R0[:], T.K0[:, 0:64], F.Copy, (), ("R0",), ("K0",))
+                    tt(Y[:, o:o + 256], YW.indirect(OF[:, o // 16:o // 16 + 16]), x1, A.subtract, ("YT", "OF" + p, xk), (yk[h],))
         elif wd[0] == "r":
-            nm = "K%d" % (k % 2)
-            tt(T["R%d" % k][:], T[nm][:, 0:64], T["R%d" % (k - 1)][:], A.min, ("R%d" % (k - 1),), ("R%d" % k,), (nm,))
-        elif wd == "w1":
-            tt(T.T3[:], T.R3[:, 0:32], T.R3[:, 32:64], A.min, ("R3",), ("T3",))
-        elif wd == "w2":
-            tt(T.T4[:], T.T3[:, 0:16], T.T3[:, 16:32], A.min, ("T3",), ("T4",))
+            ts(D[:, ck], Y[:, ck], 0.0, 2.0, A.max, A.mult, yk, dk)
+        elif wd[0] == "z":
+            mm(T["P%d" % k][:, 0:128], T.ZZ[0:32, :], T.ZZ[0:32, :], True, False, ("ZZ",), "P%d" % k)
+        elif wd[0] in "st" and k is not None:
+            j0, j1 = (int(wd[2]), int(wd[3])) if len(wd) == 4 else (int(wd[2]), int(wd[2]) + 1)
+            src, nm, t = (D, "D" + d, 0) if wd[0] == "s" else (Y, "Y" + p, 1)
+            keys = ["BB%d" % t] + ["%s%d%s" % (nm, 4 * k + j, h) for j in range(j0, j1) for h in "ab"]
+            mark = tuple("P%d_%d" % (k, j) for j in range(j0, j1))
+            for q in range(16):
+                mm(T["P%d" % k][32 * j0:32 * j1, q:128:16], src[:, 2048 * k + 512 * j0 + q:2048 * k + 512 * j1:16], T.BB[:, 8 * t:8 * t + 8],
+                   False, q == 15 and wd[0] == "s", keys, "P%d" % k, mark if q == 0 else ())
+        elif wd[0] == "c":
+            if COPY[k] == "a":
+                act(T["S%d" % k][:], T["P%d" % k][:, 0:128], F.Identity, (), ("S%d" % k,), ("P%d" % k,), bias=-2040.0)
+            else:
+                ts(T["S%d" % k][:], T["P%d" % k][:, 0:128], -2040.0, None, A.add, None, (), ("S%d" % k,), ("P%d" % k,))
+        elif wd == "k0":
+            mm(T.K[:, 0:256], T.LH[0:66, lc], T.E[0:66, 256:512], True, False, ("LH%d" % l, "E1"), "K")
+            for t in range(2):
+                mm(T.K[:, 0:256], T.ON[0:1, :], T.MM[0:1, 256 * t:256 * t + 256], False, False, ("ON", "MM%d" % t), "K")
+            mm(T.K[:, 0:256], T.IK[:], HF[:], False, False, ("IK", "HF" + p), "K")
+        elif wd in ("k1", "k2"):
+            mm(T.K[:, k - 1:256:2], T["S%d" % (k - 1)][:], T.PM[:], False, k == 2, ("S%d" % (k - 1), "PM"), "K")
+        elif wd == "sc":
+            op("v", lambda q: q.tensor_tensor_scan(T.KS[:], T.RS[:], T.K[:, 0:256], 0.0, A.add, A.min), ("RS",), ("KS",), ("K",))
         elif wd == "w3":
-            ts(T.T5[:], T.T4[:], MAGIC, -MAGIC, A.add, A.add, ("T4",), ("T5",))
+            ts(T.T5[:], T.KS[:, 15:256:16], MAGIC, -MAGIC, A.add, A.add, ("KS",), ("T5",))
         elif wd == "w4":
-            tok = tt(slot(T, s, l, 0), T.T4[:], T.T5[:], A.subtract, ("T4", "T5"), (wk,))
+            tok = tt(slot(T, s, l, 0), T.KS[:, 15:256:16], T.T5[:], A.subtract, ("KS", "T5"), (wk,))
             if l == 3:
                 return
             need("g", [tok])
@@ -347,72 +413,25 @@ def rank_program(g, core, T, topo):
                                             remote_sem=T.sem["arr%d%d" % (s, l)], src=slot(T, s, l, 0), dst=slot(T, s, l, b)))
             g.remote_dma_fused(tr, local_sem=T.sem.sent)
         elif wd == "wo":
-            ts(T.WO[:], slot(T, s, l, 0), CEN, None, A.add, None, (wk,), ("WO",))
+            ts(T.WO[:, wo], slot(T, s, l, 0), CEN, None, A.add, None, (wk,), ("WO%d" % i,))
         elif wd == "ld":
-            tt(T.LD[:], YW.indirect(T.WO[:, 0:16]), x1, A.subtract, ("YT", "WO", xk[0]), ("LD",))
+            tt(T.LD[:], YW.indirect(T.WO[:, wo]), x1, A.subtract, ("YT", "WO%d" % i, xk), ("LD",))
+            if l == 3:
+                c = slice(64 * s, 64 * s + 64)
+                cp(T.AR[:, c], T.WO[:, c], ["WO%d" % j for j in range(s, 8, 2)], ("AR%d" % s,))
+                store("s", T.argm[:, c], T.AR[:, c], ("AR%d" % s,))
         elif wd == "la":
             c = slice(256 * l, 256 * l + 256)
             if s == 0:
                 act(T.X2[:, c], T.LD[:], F.Abs, ("LD",), ("X2_%d" % l,))
             else:
                 act(T.XO[:, c], T.LD[:], F.Abs, ("LD",), ("XO%d" % l,))
-                store("s", T.xo[:, c], T.XO[:, c], ("XO%d" % l,))
-        elif wd == "ar":
-            act(T.AR[:, 64 * s + 16 * l:64 * s + 16 * l + 16], slot(T, s, l, 0), F.Identity, (wk,), ("AR%d%d" % (s, l),), bias=CEN)
-            if l == 3:
-                store("s" if s == 0 else "a", T.argm[:, 64 * s:64 * s + 64], T.AR[:, 64 * s:64 * s + 64], ["AR%d%d" % (s, j) for j in range(4)])
-        elif wd == "ib":
-            ts(T.IB[:], JJ, P, None, A.is_equal, None, ("J", "PC"), ("IB",))
-        elif wd == "ni":
-            ts(T.NI[:], JJ, P, -1.0, A.is_equal, A.mult, ("J", "PC"), ("NI",))
-        elif wd == "lm":
-            cp(T.LH[64:80, 128:512], T.K1[0:16, 128:512], (), ("LHm1",), ("K1",))
-        elif wd == "xb":
-            cp(T.X1[:, 256:512], T.X1[:, 0:256], ("X1_0a",), ("X1_0b",))
-        elif wd == "ik":
-            ts(T.IK[:], JJ, P, 4096.0, A.is_equal, A.mult, ("J", "PC"), ("IK",))
-        elif wd == "zs":
-            ts(T.ZS[:], T.J[:], GP, 4096.0, A.is_equal, A.mult, ("J", "PC"), ("ZS",))
-        elif wd == "h1":
-            ts(T.H4[:], T.HI[:], 15, None, AND, None, ("HI",), ("H4",))
-        elif wd == "h2":
-            ts(T.I16[:], T.J[:, 15:31], P15, None, A.is_equal, None, ("J", "PC"), ("I16",))
-        elif wd == "h3":
-            cp(T.HR[:], T.H4[:], ("H4",), ("HR",))
-        elif wd == "h4":
-            ts(T.H1[:], T.HI[:], 4, 15, SHR, AND, ("HI",), ("H1",))
-        elif wd == "h5":
-            ts(T.H2[:], T.HI[:], 8, None, SHR, None, ("HI",), ("H2",))
-        elif wd == "h6":
-            ts(T.H3[:], T.HI[:], 10, None, SHR, None, ("HI",), ("H3",))
-        elif wd == "h7":
-            ts(T.H2[:], T.H2[:], 48.0, None, A.mult, None, ("H2",), ("H2",))
-        elif wd == "h8":
-            ts(T.H3[:], T.H3[:], -176.0, None, A.mult, None, ("H3",), ("H3",))
-        elif wd == "h9":
-            tt(T.H1[:], T.H1[:], T.H2[:], A.add, ("H1", "H2"), ("H1",))
-        elif wd == "hA":
-            tt(T.H1[:], T.H1[:], T.H3[:], A.add, ("H1", "H3"), ("H1",))
-        elif wd == "hB":
-            cp(T.HO[:], T.H1[:], ("H1",), ("HO",))
-        elif wd == "hC":
-            ts(T.BO[:], T.J16[:], GP, None, A.is_equal, None, ("J16", "PC"), ("BO",))
-        elif wd == "hD":
-            ts(T.BG[:], T.J[:, 15:143:16], GP, None, A.is_equal, None, ("J", "PC"), ("BG",))
-        elif wd[0] == "s":
-            act(T.RD[:, k:1536:16], T.HR[:], F.Identity, ("HR", "I16"), ("RD%d" % k,), scale=T.I16[:, k:k + 1])
-        elif wd[0] == "m":
-            nm = ("PU", "PV", "PZ")[k]
-            mm(T[nm][:], T.BO[:], T.RD[:, 512 * k:512 * k + 512], True, True, ["BO"] + ["RD%d" % q for q in range(16)], nm)
-        elif wd[0] == "e":
-            nm = ("PU", "PV", "PZ")[k]
-            ts(T.MK[:, 512 * k:512 * k + 512], T[nm][:], P15, None, A.is_equal, None, ("PC",), ("MK%d" % k,), (nm,))
+                store("s" if l < 3 else "a", T.xo[:, c], T.XO[:, c], ("XO%d" % l,))
         else:
             raise ValueError(wd)
 
-    for word in ORDER.split():
-        wd, i = word.split(".")
-        piece(wd, int(i))
+    for wd, i in pieces:
+        piece(wd, i)
 
     g.wait_ge(T.sem.sent, 6 * (len(my_masks[0]) + len(my_masks[1])))
     for e in ("v", "a", "p", "g"):

from concourse.bass import DstId, RemoteDMATransfer
from concourse.mybir import AluOpType as A, ActivationFunctionType as F

KINDS = ["BBCCBBCC"] * 8
COPY = "aa"
HFON = "a"
CYCLE = """
a6.1 c0.1 mb.2 lh.2 s103.1 ez.2 of.2 c1.1 k1.1 k2.1 sc.1 w3.1 g3.2 g2.2 hm.2 w4.1 p3.2 d5.2 z1.2 wo.1 d4.2 ey.2 g6.2 p2.2
p6.2 ha.2 g7.2 zu.3 hf.2 d1.2 t102.2 k0.2 d0.2 r5.2 r4.2 r0.2 r1.2 a2.2 a3.2 z0.2 a6.2 ld.1 t002.2 p7.2 ga.3 a7.2 s004.2
hi.3 ky.4 gb.3 s103.2 c0.2 la.1 ma.3 s13.2 mb.3 k1.2 c1.2 lh.3 k2.2 ey.3 sc.2 ez.3 e1.4 ha.3 m2.3 z0.3 w3.2 of.3 z1.3
w4.2 g2.3 wo.2 ld.2 la.2 p2.3 d1.3 g6.3 d0.3 d4.3 p6.3 t002.3 hf.3 r1.3 sg.4 g3.3 g7.3 d5.3 p3.3 r0.3 m1.3 a2.3 r4.3
k0.3 p7.3 t102.3 zu.4 a3.3 ga.4 m3.3 s004.3 ma.4 gb.4 r5.3 a7.3 s13.3
"""
CEN = 1536.0
MAGIC = 1.5 * 2.0 ** 35
WHOLE = 1.5 * 2.0 ** 23


def _sb(n, d):
    return ("sbuf", [128, n], d)


SCRATCH = {
    "YT": _sb(3072, "bfloat16"), "X1": _sb(2048, "bfloat16"), "X2": _sb(1024, "bfloat16"),
    "XO": _sb(1024, "float32"), "AR": _sb(128, "float32"),
    "D0": _sb(4096, "bfloat16"), "D1": _sb(4096, "bfloat16"), "Y0": _sb(4096, "bfloat16"), "Y1": _sb(4096, "bfloat16"),
    "OF0": _sb(256, "uint16"), "OF1": _sb(256, "uint16"),
    "HF0": _sb(256, "float16"), "HF1": _sb(256, "float16"), "XZ": _sb(256, "float32"),
    "W0": _sb(192, "float32"), "W1": _sb(192, "float32"), "G": _sb(512, "float16"), "LH": _sb(512, "float16"),
    "S0": _sb(128, "float16"), "S1": _sb(128, "float16"), "KS": _sb(256, "float32"), "T5": _sb(16, "float32"),
    "WO": _sb(128, "uint16"), "LD": _sb(256, "bfloat16"),
    "BR": _sb(32, "int32"), "BR16": _sb(48, "float16"), "HM": _sb(64, "int32"), "HM16": _sb(64, "float16"),
    "HI": _sb(96, "int32"), "H1": _sb(96, "int32"), "H2": _sb(96, "int32"), "H3": _sb(96, "int32"), "HX": _sb(192, "int32"),
    "HO": _sb(192, "uint16"), "MK": _sb(1536, "bfloat16"),
    "PI": _sb(4, "int32"), "PC": _sb(4, "float32"), "AB": _sb(8, "float32"),
    "J": _sb(128, "bfloat16"), "JP": _sb(128, "bfloat16"), "EJ": _sb(512, "bfloat16"), "CJ": _sb(256, "bfloat16"),
    "EW": _sb(512, "float16"), "ED": _sb(512, "float16"), "E": _sb(512, "float16"),
    "IH": _sb(128, "float16"), "IK": _sb(128, "float16"), "IB": _sb(128, "bfloat16"), "NI": _sb(128, "bfloat16"),
    "PM": _sb(128, "float16"), "BH": _sb(16, "float16"), "BB": _sb(16, "bfloat16"), "I16": _sb(16, "bfloat16"),
    "ZZ": _sb(128, "bfloat16"), "RS": _sb(256, "bfloat16"), "ON": _sb(128, "bfloat16"), "MM": _sb(512, "bfloat16"),
}
for _n in ("P0", "P1", "K", "PU", "PZ", "PD0", "PD1", "PD2"):
    SCRATCH[_n] = ("psum", [128, 512], "float32")
SEMAPHORES = ["cv", "ca", "cp", "cg", "lbr", "lhm", "ly", "lx0", "lhi", "lx1", "st", "sent"] + \
             ["arr%d%d" % (s, l) for s in range(2) for l in range(3)]


def routes(T, topo):
    cores = list(T.cores)
    n = len(cores)
    taken = []
    out = []
    for r in range(n):
        src = cores[r]
        ways = []
        for b in (1, 2):
            dst = cores[(r - b) % n]
            if topo.may_write(src, dst):
                ways.append((dst, dst, b))
                continue
            cand = [c for c in topo.cores_of(src) if c not in cores and c not in taken and topo.may_write(c, dst)]
            cand.sort(key=lambda c: (topo.die(c) != topo.die(src), c))
            taken.append(cand[0])
            ways.append((cand[0], dst, b))
        out.append(ways)
    return out


def bits(engines):
    m = 0
    for e in engines:
        m |= 1 << e
    return m


def first_hop_masks(src, ways, topo):
    a, b = topo.engines(src, ways[0][0]), topo.engines(src, ways[1][0])
    both = [e for e in a if e in b]
    h = len(both) // 2
    return [both[:h], both[h:2 * h]]


def slot(T, s, l, b):
    return T["W%d" % s][:, 48 * l + 16 * b:48 * l + 16 * b + 16]


def relay_program(g, core, T, topo, src, ways, k):
    _, dst, b = ways[k]
    n_in = len(first_hop_masks(src, ways, topo)[k])
    rid, pid = topo.addr(dst, core)
    n_out = len(topo.engines(core, dst))
    for l in range(3):
        for s in range(2):
            sem = T.sem["arr%d%d" % (s, l)]
            g.wait_ge(sem, n_in)
            g.remote_dma(slot(T, s, l, b), slot(T, s, l, b), sem, T.sem.sent, pid, rid, topo.mask(core, dst))
    g.wait_ge(T.sem.sent, 6 * n_out)


def order():
    words = [wd.split(".") for wd in CYCLE.split()]
    return [(wd, n + int(j)) for n in range(-6, 14, 2) for wd, j in words if 0 <= n + int(j) < 8]


def rank_program(g, core, T, topo):
    rank = T.rank_of(core)
    plan = routes(T, topo)
    cores = list(T.cores)
    if rank is None:
        for r, ways in enumerate(plan):
            for k in range(2):
                if ways[k][0] == core:
                    relay_program(g, core, T, topo, cores[r], ways, k)
        return

    n_arr = 0
    for r, ways in enumerate(plan):
        for k in range(2):
            first, dst, _ = ways[k]
            if dst == core:
                n_arr += len(first_hop_masks(cores[r], ways, topo)[k]) if first == dst else len(topo.engines(first, dst))
    my_ways = plan[rank]
    my_masks = first_hop_masks(core, my_ways, topo)

    Q = {"v": g.vector, "a": g.scalar, "p": g.tensor, "g": g, "s": g.sync}
    CS = {"v": "cv", "a": "ca", "p": "cp", "g": "cg"}
    count = {"v": 0, "a": 0, "p": 0, "g": 0}
    waited = {k: {} for k in Q}
    last_w, readers, bank = {}, {}, {}
    stores = [0]

    def need(eng, deps):
        best = {}
        for (e, sem, val) in deps:
            if e == "p" and eng == "p":
                continue
            best[sem] = max(best.get(sem, 0), val)
        for sem, val in best.items():
            if waited[eng].get(sem, 0) < val:
                Q[eng].wait_ge(T.sem[sem], val)
                waited[eng][sem] = val

    def deps_of(eng, r, w, banks, extra):
        deps = list(extra)
        for k in r:
            deps.append(last_w[k])
        for k in w:
            if k in last_w:
                deps.append(last_w[k])
            deps.extend(readers.get(k, []))
        for k in banks:
            for e, t in bank.get(k, {}).items():
                if e != eng:
                    deps.append(t)
        return deps

    def op(eng, fn, r=(), w=(), banks=(), extra=()):
        need(eng, deps_of(eng, r, w, banks, extra))
        count[eng] += 1
        fn(Q[eng]).then_inc(T.sem[CS[eng]], 1)
        tok = (eng, CS[eng], count[eng])
        for k in r:
            readers.setdefault(k, []).append(tok)
        for k in w:
            last_w[k] = tok
            readers[k] = []
        for k in banks:
            bank.setdefault(k, {})[eng] = tok
        return tok

    def load(eng, out, in_, sem, total, key):
        Q[eng].dma_start(out, in_).then_inc(T.sem[sem], 16)
        last_w[key] = ("d", sem, total)

    def store(eng, out, in_, r):
        need(eng, deps_of(eng, r, (), (), ()))
        Q[eng].dma_start(out, in_).then_inc(T.sem.st, 16)
        stores[0] += 16

    def ts(out, in0, s1, s2, op0, op1, r, w, banks=()):
        if op1 is None:
            return op("v", lambda q: q.tensor_scalar(out, in0, s1, None, op0), r, w, banks)
        return op("v", lambda q: q.tensor_scalar(out, in0, s1, s2, op0, op1), r, w, banks)

    def tt(out, in0, in1, o, r, w, banks=(), extra=()):
        return op("v", lambda q: q.tensor_tensor(out, in0, in1, o), r, w, banks, extra)

    def cp(out, in_, r, w, banks=()):
        return op("v", lambda q: q.tensor_copy(out, in_), r, w, banks)

    def fill(out, v, w, r=()):
        return op("v", lambda q: q.memset(out, v), r, w)

    def act(out, in_, func, r, w, banks=(), bias=0.0, scale=1.0):
        return op("a", lambda q: q.activation(out, in_, func, bias=bias, scale=scale), r, w, banks)

    def mm(out, lhsT, rhs, start, stop, r, bk, w=()):
        return op("p", lambda q: q.matmul(out, lhsT, rhs, start, stop), r, w, (bk,))

    def iota(out, pat, base, cm, key, small=True):
        if small:
            return op("g", lambda q: q.iota(out, pat, base, cm, allow_small_or_imprecise_dtypes=True), (), (key,))
        return op("g", lambda q: q.iota(out, pat, base, cm), (), (key,))

    load("s", T.BR[:, 0:16], T.lo0[:], "lbr", 32, "BR")
    load("a", T.BR[:, 16:32], T.hi0[:], "lbr", 32, "BR")
    load("a", T.X1[:, 0:256], T.xrow[:, 0:256], "lx0", 16, "X0")
    load("s", T.YT[:], T.ytab[:], "ly", 16, "YT")
    load("a", T.HM[:], T.home[:], "lhm", 16, "HM")
    for l in range(3):
        for t, src in enumerate((T.ha, T.hb)):
            load("s", T.HI[:, 32 * l + 16 * t:32 * l + 16 * t + 16], src[:, 16 * l:16 * l + 16], "lhi", 96, "HI")
    for l in range(1, 4):
        for h in range(2):
            load("s", T.X1[:, 512 * l + 256 * h:512 * l + 256 * h + 256], T.xrow[:, 256 * l:256 * l + 256], "lx1", 96,
                 "X1_%d" % l)

    SHR, AND = A.logical_shift_right, A.bitwise_and
    iota(T.PI[:], [[0, 4]], 0, 1, "PI", small=False)
    iota(T.J[:], [[1, 128]], 0, 0, "J")
    iota(T.EJ[:, 256:512], [[0, 16], [1, 16]], 0, 0, "EJ1")
    iota(T.EJ[:, 0:256], [[1, 2], [2, 8], [0, 16]], 0, 0, "EJ0")
    iota(T.CJ[:], [[1, 16], [0, 16]], 0, 0, "CJ")
    iota(T.JP[:], [[1, 16], [16, 8]], 0, 0, "JP")
    LHK = ["LH%d" % l for l in range(4)]
    fill(T.AB[:], 0.0, ("AB",))
    fill(T.LH[:], 0.0, LHK + ["LHm"])
    for c, m in ((1, 16), (2, 112), (3, 15)):
        ts(T.PI[:, c:c + 1], T.PI[:, 0:1], m, None, AND, None, ("PI",), ("PI%d" % c,))
    AB = ["AB%d" % k for k in range(11)]
    for k, (p0, p1, c, v) in enumerate(((64, 96, 1, -15 / 32), (32, 64, 0, 1 / 8), (32, 64, 1, -1.0), (96, 128, 1, -1.0), (64, 96, 2, 1.0),
                                        (0, 32, 3, -4096.0), (32, 64, 4, -CEN), (64, 65, 0, CEN / 8), (64, 65, 1, -CEN))):
        fill(T.AB[p0:p1, c:c + 1], v, (AB[k],), ("AB", "AB0") if k == 8 else ("AB",))
        if k == 4:
            cp(T.PC[:], T.PI[:], ("PI", "PI1", "PI2", "PI3"), ("PC",))
    P, GP, P15 = T.PC[:, 0:1], T.PC[:, 2:3], T.PC[:, 3:4]
    ts(T.AB[0:32, 0:1], T.PC[0:32, 1:2], 1 / 128, -1 / 16, A.mult, A.add, ("PC", "AB"), (AB[9],))
    ts(T.AB[0:32, 1:2], T.PC[0:32, 1:2], -1 / 16, 1.0, A.mult, A.add, ("PC", "AB"), (AB[10],))
    ts(T.IH[:], T.J[:], P, None, A.is_equal, None, ("J", "PC"), ("IH",))
    fill(T.LH[64:66, :], 1.0, LHK)
    fill(T.BR16[:, 32:48], 0.0, ("BR0",))

    def weights(h):
        c = slice(256 * h, 256 * h + 256)
        act(T.EW[:, c], T.EJ[:, c], F.Identity, ["EJ%d" % h] + AB, ("EW%d" % h,), bias=T.AB[:, 1:2], scale=T.AB[:, 0:1])
        ts(T.ED[:, c], (T.EJ[:, 256:512], T.CJ[:])[h], P15, T.AB[:, 2:3], A.is_equal, A.max, [("EJ1", "CJ")[h], "PC"] + AB, ("ED%d" % h,))
        tt(T.E[:, c], T.EW[:, c], T.ED[:, c], A.mult, ("EW%d" % h, "ED%d" % h), ("E%d" % h,))

    weights(0)
    ts(T.BR16[:, 0:32], T.BR[:], -CEN, None, A.add, None, ("BR",), ("BR16",))
    mm(T.PU[0:48, 0:128], T.BR16[:], T.IH[:], True, True, ("BR16", "BR0", "IH"), "PU")

    def homes():
        ts(T.HM16[:], T.HM[:], -CEN, None, A.add, None, ("HM",), ("HM16",))
        for l in range(4):
            mm(T.K[0:16, 128 * l:128 * l + 128], T.HM16[:, 16 * l:16 * l + 16], T.IH[:], True, True, ("HM16", "IH"), "K")
        act(T.LH[96:112, :], T.K[0:16, :], F.Copy, (), ("LHm",), ("K",))

    def signs():
        ts(T.IB[:], T.J[:], P, None, A.is_equal, None, ("J", "PC"), ("IB",))
        act(T.NI[:], T.IH[:], F.Copy, ("IH",), ("NI",), scale=-1.0)
        fill(T.ZZ[:], 0.0, ("ZZ",))
        cp(T.X1[:, 256:512], T.X1[:, 0:256], ("X0",), ("X1_0",))
        for t in range(2):
            ts(T.BB[:, 8 * t:8 * t + 8], T.J[:, 0:128:16], GP, 1.0 - 2 * t, A.is_equal, A.mult, ("J", "PC"), ("BB%d" % t,))

    def keyed():
        act(T.IK[:], T.IH[:], F.Copy, ("IH",), ("IK",), scale=4096.0)
        ts(T.PM[:], T.JP[:], P, 4096.0, A.is_equal, A.mult, ("JP", "PC"), ("PM",))
        ts(T.RS[:], T.EJ[:, 256:512], 0.0, 2.0 ** 25, A.is_equal, A.mult, ("EJ1",), ("RS",))
        fill(T.ON[0:1, :], 1.0, ("ON",))
        fill(T.MM[0:1, 0:256], WHOLE, ("MM0",))
        fill(T.MM[0:1, 256:512], -WHOLE, ("MM1",))

    def hints():
        ts(T.H1[:], T.HI[:], 2, 192, SHR, AND, ("HI",), ("H1",))
        ts(T.H2[:], T.HI[:], 6, 48, SHR, AND, ("HI",), ("H2",))
        ts(T.H3[:], T.HI[:], 4, 15, SHR, AND, ("HI",), ("H3",))
        ts(T.HX[:, 96:192], T.HI[:], 15, None, AND, None, ("HI",), ("HQ",))
        ts(T.H1[:], T.H1[:], 0.75, None, A.mult, None, ("H1",), ("H1",))
        tt(T.H2[:], T.H2[:], T.H3[:], A.add, ("H2", "H3"), ("H2",))
        ts(T.I16[:], T.J[:, 0:16], P15, None, A.is_equal, None, ("J", "PC"), ("I16",))
        tt(T.HX[:, 0:96], T.H1[:], T.H2[:], A.add, ("H1", "H2"), ("HX",))
        act(T.BH[:], T.BB[:], F.Copy, ("BB0", "BB1"), ("BH",))
        cp(T.HO[:], T.HX[:], ("HX", "HQ"), ("HO",))

    def mask(l):
        act(T.MK[:, 512 * l - 512:512 * l], T.I16[:, 0:16].indirect(T.HO[:, 64 + 32 * l:96 + 32 * l]), F.Copy, ("I16", "HO"), ("MK%d" % l,))

    steps = [(s, l) for l in range(4) for s in range(2)]
    YW = T.YT[:, 0:3072]
    pieces = order()
    pd = [(i, k) for i in range(8) for k in range(8) if KINDS[i][k] == "C"]
    pd = {c: "PD%d" % (n % 3) for n, c in enumerate(pd)}
    once = {"e1": (0, lambda: weights(1)), "hm": (0, homes), "sg": (0, signs), "ky": (0, keyed), "hi": (1, hints),
            "m1": (1, lambda: mask(1)), "m2": (1, lambda: mask(2)), "m3": (1, lambda: mask(3))}

    def piece(wd, i):
        s, l = steps[i]
        p = "0" if i < 2 else "%d" % ((i + 1) % 2)
        d = "%d" % (i % 2)
        OF, HF, Y, D = T["OF" + p], T["HF" + p], T["Y" + p], T["D" + d]
        lc = slice(128 * l, 128 * l + 128)
        if s == 0:
            x1, x2, xk = T.X1[:, 512 * l:512 * l + 256], T.X1[:, 512 * l:512 * l + 512], "X1_%d" % l
        else:
            x1, x2, xk = T.X2[:, 256 * l:256 * l + 256], None, "X2_%d" % l
        wk = "W%d%d" % (s, l)
        wo = slice(64 * s + 16 * l, 64 * s + 16 * l + 16)
        if wd in once:
            if i == once[wd][0]:
                once[wd][1]()
            return
        k = int(wd[1]) if wd[1].isdigit() else None
        kind = KINDS[i][k] if wd[0] in "gpadr" and k is not None else None
        if i < 2 and wd in ("zu", "ga", "gb", "ma", "mb") or \
                i == 1 and (wd in ("lh", "ez", "ey", "of", "ha", "hf") or wd[0] == "g" and KINDS[0][k] == "C"):
            return
        if kind is not None:
            k1 = int(wd[-1]) + 1
            ck = slice(512 * k, 512 * k1)
            yk, dk = (tuple("%s%d%s" % (nm, j, h) for j in range(k, k1) for h in "ab") for nm in ("Y" + p, "D" + d))
        if wd == "zu":
            mm(T.PU[0:48, 0:128], T.ZZ[0:32, 0:48], T.ZZ[0:32, :], True, False, ("ZZ",), "PU")
        elif wd in ("ga", "gb"):
            t = "ab".index(wd[1])
            c0 = 512 * (l - 1) + 256 * t
            win = T["W%d" % s][:, 0:48 * l].indirect(T.HO[:, c0 // 16:c0 // 16 + 16])
            tt(T.G[:, 256 * t:256 * t + 256], win, T.MK[:, c0:c0 + 256], A.mult, ["HO", "MK%d" % l] + ["W%d%d" % (s, j) for j in range(l)],
               ("G%d" % t,), extra=[("d", "arr%d%d" % (s, l - 1), n_arr)])
        elif wd == "ma":
            for q in range(16):
                mm(T.PU[32:48, q:128:16], T.G[:, q:256:16], T.BH[:, 0:8], False, False, ("G0", "BH"), "PU")
        elif wd == "mb":
            for q in range(16):
                mm(T.PU[32:48, q:128:16], T.G[:, 256 + q:512:16], T.BH[:, 8:16], False, q == 15, ("G1", "BH"), "PU")
                mm(T.PU[0:32, q:128:16], T.G[:, q:512:16], T.BH[:, 0:8], False, q == 15, ("G0", "G1", "BH"), "PU")
        elif wd == "lh":
            ts(T.LH[0:48, lc], T.PU[0:48, 0:128], T.AB[0:48, 3:4], T.AB[0:48, 4:5], A.max, A.add, AB, ("LH%d" % l,), ("PU",))
        elif wd == "ez":
            mm(T.PZ[:, 0:256], T.LH[0:66, lc], T.E[0:66, 0:256], True, True, ("LH%d" % l, "E0"), "PZ")
        elif wd == "ey":
            mm(T.PU[:, 128:384], T.LH[0:112, lc], T.E[0:112, 256:512], True, True, ("LH%d" % l, "LHm", "E1"), "PU")
        elif wd == "of":
            ts(OF[:], T.PZ[:, 0:256], CEN, None, A.add, None, (), ("OF" + p,), ("PZ",))
        elif wd == "ha":
            act(T.XZ[:], T.PU[:, 128:384], F.Abs, (), ("XZ",), ("PU",), scale=1 / 16)
        elif wd == "hf":
            if HFON == "a":
                act(HF[:], T.XZ[:], F.Identity, ("XZ",), ("HF" + p,), bias=-2047 - 15 / 32)
            else:
                ts(HF[:], T.XZ[:], -2047 - 15 / 32, None, A.add, None, ("XZ",), ("HF" + p,))
        elif wd[0] == "g":
            act(Y[:, ck], YW.indirect(OF[:, 32 * k:32 * k1]), F.Copy, ("YT", "OF" + p), yk)
        elif wd[0] == "p":
            nm = pd[i, k]
            mm(T[nm][:], T.IB[:], Y[:, ck], True, False, ("IB",) + yk, nm)
            if s == 0:
                mm(T[nm][:], T.NI[:], x2, False, True, ("NI", xk), nm)
            else:
                mm(T[nm][:, 0:256], T.NI[:], x1, False, False, ("NI", xk), nm)
                mm(T[nm][:, 256:512], T.NI[:], x1, False, True, ("NI", xk), nm)
        elif wd[0] == "a":
            if kind == "C":
                act(D[:, ck], T[pd[i, k]][:], F.Abs, (), dk, (pd[i, k],))
            else:
                act(D[:, ck], Y[:, ck], F.Abs, yk, dk)
        elif wd[0] == "d":
            if s == 0:
                tt(Y[:, ck], YW.indirect(OF[:, 32 * k:32 * k + 32]), x2, A.subtract, ("YT", "OF" + p, xk), yk)
            else:
                for h in range(2):
                    o = 512 * k + 256 * h
                    tt(Y[:, o:o + 256], YW.indirect(OF[:, o // 16:o // 16 + 16]), x1, A.subtract, ("YT", "OF" + p, xk), (yk[h],))
        elif wd[0] == "r":
            ts(D[:, ck], Y[:, ck], 0.0, 2.0, A.max, A.mult, yk, dk)
        elif wd[0] == "z":
            mm(T["P%d" % k][:, 0:128], T.ZZ[0:32, :], T.ZZ[0:32, :], True, False, ("ZZ",), "P%d" % k)
        elif wd[0] in "st" and k is not None:
            j0, j1 = (int(wd[2]), int(wd[3])) if len(wd) == 4 else (int(wd[2]), int(wd[2]) + 1)
            src, nm, t = (D, "D" + d, 0) if wd[0] == "s" else (Y, "Y" + p, 1)
            keys = ["BB%d" % t] + ["%s%d%s" % (nm, 4 * k + j, h) for j in range(j0, j1) for h in "ab"]
            mark = tuple("P%d_%d" % (k, j) for j in range(j0, j1))
            for q in range(16):
                mm(T["P%d" % k][32 * j0:32 * j1, q:128:16], src[:, 2048 * k + 512 * j0 + q:2048 * k + 512 * j1:16], T.BB[:, 8 * t:8 * t + 8],
                   False, q == 15 and wd[0] == "s", keys, "P%d" % k, mark if q == 0 else ())
        elif wd[0] == "c":
            if COPY[k] == "a":
                act(T["S%d" % k][:], T["P%d" % k][:, 0:128], F.Identity, (), ("S%d" % k,), ("P%d" % k,), bias=-2040.0)
            else:
                ts(T["S%d" % k][:], T["P%d" % k][:, 0:128], -2040.0, None, A.add, None, (), ("S%d" % k,), ("P%d" % k,))
        elif wd == "k0":
            mm(T.K[:, 0:256], T.LH[0:66, lc], T.E[0:66, 256:512], True, False, ("LH%d" % l, "E1"), "K")
            for t in range(2):
                mm(T.K[:, 0:256], T.ON[0:1, :], T.MM[0:1, 256 * t:256 * t + 256], False, False, ("ON", "MM%d" % t), "K")
            mm(T.K[:, 0:256], T.IK[:], HF[:], False, False, ("IK", "HF" + p), "K")
        elif wd in ("k1", "k2"):
            mm(T.K[:, k - 1:256:2], T["S%d" % (k - 1)][:], T.PM[:], False, k == 2, ("S%d" % (k - 1), "PM"), "K")
        elif wd == "sc":
            op("v", lambda q: q.tensor_tensor_scan(T.KS[:], T.RS[:], T.K[:, 0:256], 0.0, A.add, A.min), ("RS",), ("KS",), ("K",))
        elif wd == "w3":
            ts(T.T5[:], T.KS[:, 15:256:16], MAGIC, -MAGIC, A.add, A.add, ("KS",), ("T5",))
        elif wd == "w4":
            tok = tt(slot(T, s, l, 0), T.KS[:, 15:256:16], T.T5[:], A.subtract, ("KS", "T5"), (wk,))
            if l == 3:
                return
            need("g", [tok])
            tr = []
            for j in range(2):
                first, dst, b = my_ways[j]
                rid, pid = topo.addr(first, core)
                tr.append(RemoteDMATransfer(dst_ids=[DstId(rid=rid, pnc=pid)], dma_engine_mask=bits(my_masks[j]),
                                            remote_sem=T.sem["arr%d%d" % (s, l)], src=slot(T, s, l, 0), dst=slot(T, s, l, b)))
            g.remote_dma_fused(tr, local_sem=T.sem.sent)
        elif wd == "wo":
            ts(T.WO[:, wo], slot(T, s, l, 0), CEN, None, A.add, None, (wk,), ("WO%d" % i,))
        elif wd == "ld":
            tt(T.LD[:], YW.indirect(T.WO[:, wo]), x1, A.subtract, ("YT", "WO%d" % i, xk), ("LD",))
            if l == 3:
                c = slice(64 * s, 64 * s + 64)
                cp(T.AR[:, c], T.WO[:, c], ["WO%d" % j for j in range(s, 8, 2)], ("AR%d" % s,))
                store("s", T.argm[:, c], T.AR[:, c], ("AR%d" % s,))
        elif wd == "la":
            c = slice(256 * l, 256 * l + 256)
            if s == 0:
                act(T.X2[:, c], T.LD[:], F.Abs, ("LD",), ("X2_%d" % l,))
            else:
                act(T.XO[:, c], T.LD[:], F.Abs, ("LD",), ("XO%d" % l,))
                store("s" if l < 3 else "a", T.xo[:, c], T.XO[:, c], ("XO%d" % l,))
        else:
            raise ValueError(wd)

    for wd, i in pieces:
        piece(wd, i)

    g.wait_ge(T.sem.sent, 6 * (len(my_masks[0]) + len(my_masks[1])))
    for e in ("v", "a", "p", "g"):
        g.wait_ge(T.sem[CS[e]], count[e])
    g.wait_ge(T.sem.st, stores[0])
